import numpy as np, ml_dtypes
CORES = [66,74,82,90,194,202,210,218]
N = 8
import mx_ref
BF = ml_dtypes.bfloat16
def cols(t, e):
    v = np.concatenate([t.reshape(128, -1, 4), np.zeros((128, 1, 4), BF)], axis=1)
    return np.ascontiguousarray(v[:, e]).reshape(128, -1)
def tile(rs):
    return np.stack(rs, axis=2).reshape(128, -1).astype(BF)
def cut(t, i, w=512):
    return t[:, w * i:w * i + w]
def f(rng, *shape):
    return mx_ref.flush((rng.standard_normal(shape, dtype=np.float32) * np.exp2(rng.integers(-2, 3, shape[:-1] + (1,)))).astype(BF))
def wide(rng, *shape, cols=0):
    v = rng.standard_normal(shape, dtype=np.float32) * np.exp2(rng.integers(-12, 13, shape)).astype(np.float32)
    if cols: v *= np.repeat(np.exp2(rng.integers(-cols, cols + 1, shape[:-2] + (1, shape[-1] // 4))) * (rng.random(shape[:-2] + (1, shape[-1] // 4)) > 0.0625), 4, axis=-1).astype(np.float32)
    return mx_ref.flush(v.astype(BF))
T, ST = 256, 128
def flags(rng, n, new):
    s = np.zeros((N, T), bool)
    for r in range(N):
        s[r, 0] = new[r] > 0
        s[r, 1 + rng.permutation(T - 1)[:int(n[r]) - int(new[r])]] = True
    return s
def borders(rng):
    new = rng.integers(0, 2, N); new[0] = 1
    return new
def make(rng, s, far=2, spread=False):
    t = np.zeros((128, 128, 4), np.float32); t[:, :16] = rng.standard_normal((128, 16, 4), dtype=np.float32)
    if spread: t[64:] = 0
    t = mx_ref.flush(t.reshape(128, 512).astype(BF))
    k = (rng.integers(0, 16) + np.cumsum(s.reshape(-1) * rng.integers(1, 16, N * T))) % 16
    c = t.astype(np.float32).reshape(128, 128, 4)[:, k] + rng.standard_normal((128, N * T, 4), dtype=np.float32) * np.float32(0.125)
    if spread: c[64:] = wide(rng, 64, 4 * N * T).astype(np.float32).reshape(64, N * T, 4)
    c = c * np.exp2(rng.integers(-far, far + 1, (N * T, 1))).astype(np.float32)
    x = np.ascontiguousarray(c.reshape(128, N, 4 * T).transpose(1, 0, 2)).astype(BF)
    return {"x": mx_ref.flush(x), "p": np.stack([t] * N), "a": f(rng, N, 128, 2048), "w": f(rng, N, 128, 512), "v": f(rng, N, 128, 512)}
def setup_inputs(rng):
    return make(rng, flags(rng, rng.integers(1, ST + 1, N), borders(rng)))
def setup_inputs_border(rng):
    return make(rng, flags(rng, rng.integers(1, ST + 1, N), np.arange(N) == 0))
def setup_inputs_dense(rng):
    n = np.full(N, ST); n[0] = ST - rng.integers(1, N)
    return make(rng, flags(rng, n, borders(rng)))
def setup_inputs_one(rng):
    return make(rng, flags(rng, np.ones(N, int), np.arange(N) == 0))
def setup_inputs_spread(rng):
    return make(rng, flags(rng, rng.integers(1, ST + 1, N), borders(rng)), far=8, spread=True)
def setup_inputs_ties(rng):
    d = setup_inputs(rng)
    m = np.cumsum(flags(rng, rng.integers(1, ST + 1, N), borders(rng)).reshape(-1)) - 1; n = int(m[-1]) + 1
    u = np.zeros((128, 8, 4), np.float32); u[:64] = rng.choice([-1, 1], (64, 8, 4)) * rng.uniform(0.75, 1.25, (64, 8, 4))
    g = np.zeros((128, 1, 4), np.float32); g[64:] = rng.choice([-1, 1], (64, 1, 4))
    t = np.zeros((128, 128, 4), np.float32); t[:, :8] = u + g; t[:, 8:16] = u + g
    k = np.cumsum(rng.integers(1, 8, n)) % 8
    big = int(np.argmax(np.bincount(m)))
    k = (k - k[big]) % 8
    neg = rng.permutation(n) % 2
    c = u[:, k[m]] + g * np.where(neg[m] > 0, -2, 1).astype(np.float32)[:, None] + rng.standard_normal((128, N * T, 4), dtype=np.float32) * np.float32(0.125)
    c = c * np.exp2(rng.integers(-2, 3, (N * T, 1))).astype(np.float32)
    zero = (k[m] == 0) & (rng.random(N * T) < 0.25); zero[np.flatnonzero(m == big)[1]] = True
    c[:, zero] = 0
    d["x"] = mx_ref.flush(np.ascontiguousarray(c.reshape(128, N, 4 * T).transpose(1, 0, 2)).astype(BF))
    d["p"] = np.stack([mx_ref.flush(t.reshape(128, 512).astype(BF))] * N)
    return d
def labels(x, p):
    return np.stack([np.argmax(mx_ref.matmul(mx_ref.quantize(p[r]), mx_ref.quantize(x[r]))[:16] + np.float32(0.0), axis=0) for r in range(N)])
def starts(l):
    e = l.reshape(-1)
    return np.concatenate([[True], e[1:] != e[:-1]])
def check_inputs(d):
    b = []
    for r in range(N):
        if not np.array_equal(d["p"][r], d["p"][0]): b.append("p (the same on all ranks)")
        if d["p"][r][:, 64:].astype(np.float32).any(): b.append("p (zero columns)")
    n = starts(labels(d["x"], d["p"])).reshape(N, T).sum(axis=1)
    if n.min() < 1 or n.max() > ST: b.append("x (runs that start on a rank)")
    return b
def reference(x, p, a, w, v):
    l = labels(x, p); s = starts(l)
    m = np.add.accumulate(s.astype(int)) - 1
    first = np.flatnonzero(s)
    seq = np.concatenate([x[r] for r in range(N)], axis=1)
    h = []
    for r in range(N):
        e = np.full(ST, -1); mine = first[r::N]; e[:len(mine)] = mine
        c = mx_ref.quantize(cols(seq, e))
        h.append(tile([np.maximum(mx_ref.matmul(mx_ref.quantize(np.ascontiguousarray(cut(a[r], i))), c), np.float32(0)) * np.float32(0.05) for i in range(4)]))
    h = np.concatenate(h, axis=1)
    y = np.zeros((N, 128, T), np.float32); lb = np.zeros((N, 2, T), np.float32)
    for r in range(N):
        k = m[r * T:r * T + T]
        hk = mx_ref.quantize(cols(h, (k % N) * ST + k // N))
        y[r] = mx_ref.matmul(mx_ref.quantize(w[r]), mx_ref.quantize(x[r])) + mx_ref.matmul(mx_ref.quantize(v[r]), hk)
        lb[r, 0] = l[r]; lb[r, 1] = k
    return {"y": y, "lb": lb}

@@ -1,0 +1,390 @@
+from concourse.bass import DstId, RemoteDMATransfer
+from concourse.mybir import dt, AluOpType as Op, AxisListType, ActivationFunctionType as Act
+
+N, TC = 8, 256
+W = 18
+RW = 20
+NB, NR = N * W, N * RW
+PAD = 112
+H0 = 4 * PAD
+LAND, RLAND = 128 + (N - 1) * W, 128 + (N - 1) * RW
+NE = 9
+NO = NE + 1
+SC = [0, 1, 2, 3, 4]
+VC = [5, 6, 7, 8]
+NV = len(VC)
+BIG = 1e29
+SB = 5
+VL = 256 - 32 * SB
+
+SCRATCH = {}
+for _n, _w, _t in (
+        ("xs", 1024, "bfloat16"), ("pst", 512, "bfloat16"), ("as_", 2048, "bfloat16"), ("ws", 512, "bfloat16"), ("vsb", 512, "bfloat16"),
+        ("tr", 256, "float32"), ("pm", 256, "float32"), ("mk1", 256, "float32"), ("eq", VL, "bfloat16"), ("ls", VL, "bfloat16"),
+        ("zr", 32, "bfloat16"), ("lab", 8, "float32"), ("sgl", 128, "bfloat16"), ("bc", 256, "bfloat16"), ("row", 256, "bfloat16"),
+        ("sf", 256, "bfloat16"), ("cum", 256, "bfloat16"), ("ones", 256, "bfloat16"), ("tpk", 8, "float32"), ("msg", 2, "uint16"),
+        ("pi", 1, "int32"), ("ii", 4, "int32"), ("fi", 4, "float32"), ("th0", NE, "float32"), ("thr", NE, "float32"), ("te", NE, "float32"),
+        ("t1", NE, "float32"), ("t2", NE, "float32"), ("t3", NE, "float32"), ("t4", NE, "float32"),
+        ("ss", NE, "float32"), ("sg", 256 * len(SC), "bfloat16"), ("cm", 256 * NV, "bfloat16"), ("cs", 256 * NV, "bfloat16"), ("of", 4 * NO, "uint16"),
+        ("ct", 64 * NE, "bfloat16"), ("q0", 36, "float32"), ("q", 36, "float32"), ("qm", 36, "int32"), ("qd", 36, "int32"), ("b1", 36, "float32"),
+        ("b2", 36, "float32"), ("b3", 36, "float32"), ("b4", 36, "float32"), ("b5", 36, "float32"), ("b6", 36, "float32"), ("base", 36, "float32"),
+        ("off", 36, "uint16"), ("info", 8, "uint16"), ("inf", 8, "int32"),
+        ("la", 8, "int32"), ("fb", 8, "int32"), ("sb", 24, "float32"), ("d0", 24, "float32"), ("so", 24, "float32"),
+        ("hs", 4 * (PAD + NB), "bfloat16"), ("hb", 4 * (PAD + NB), "bfloat16"),
+        ("jm", 256, "float32"), ("m16", 256, "bfloat16"), ("rm", 256, "bfloat16"), ("cw0", 256, "bfloat16"), ("cw1", 256, "bfloat16"),
+        ("bt", 4, "float32"), ("gi", 16, "int32"), ("gr", 16, "int32"), ("h1", 16, "int32"), ("d1", 16, "int32"), ("z", 16, "float32"),
+        ("u", 16, "float32"), ("u2", 16, "float32"), ("u3", 16, "float32"), ("pos", 16, "uint16"), ("ni", 8, "int32"), ("nf", 16, "float32"),
+        ("lbt", 512, "float32"), ("wy", 256, "float32"), ("vw", NR, "float32"), ("yt", 256, "float32")):
+    SCRATCH[_n] = ("sbuf", [128, _w], _t)
+for _n, _m, _w in (("pc", "pp", 128), ("xc", "xp", 256), ("ac", "apl", 512), ("wc", "wp", 128), ("vc", "vp", 128),
+                   ("sc", "sp", NB), ("fc", "fp", LAND), ("hc", "hp", NB), ("rc", "rp", RLAND)):
+    SCRATCH[_n] = ("sbuf", [128, _w], "float8_e4m3fn_x4")
+    SCRATCH[_m] = ("sbuf", [128, _w], "uint8")
+for _i in range(8):
+    SCRATCH["ps%d" % _i] = ("psum", [128, 512], "float32")
+SEMAPHORES = ["v", "s", "t", "gc", "lp", "lxa", "lxb", "la_", "lw", "lv", "inf_", "ae", "af", "ar", "loc", "sy0", "sy1", "slb"]
+
+
+def rank_program(g, core, T, topo):
+    r = T.rank_of(core)
+    if r is None:
+        return
+    V, S, E, Y = g.vector, g.scalar, g.tensor, g.sync
+    queues = {"v": V, "s": S, "t": E, "y": Y, "g": g}
+    cnt, seen = {}, {}
+    early = 2 if r == N - 1 else 0
+
+    def inc(ins, sem, n=1):
+        ins.then_inc(T.sem[sem], n)
+        cnt[sem] = cnt.get(sem, 0) + n
+        return (sem, cnt[sem])
+
+    def need(q, *toks):
+        best = {}
+        for s, n in toks:
+            best[s] = max(best.get(s, 0), n)
+        for s, n in best.items():
+            if seen.get((q, s), 0) < n:
+                seen[(q, s)] = n
+                queues[q].wait_ge(T.sem[s], n)
+
+    def v(ins): return inc(ins, "v")
+    def s_(ins): return inc(ins, "s")
+    def t_(ins): return inc(ins, "t")
+    def gc(ins): return inc(ins, "gc")
+
+    others = [(r + k) % N for k in range(1, N)]
+    mask = topo.mask(core, T.cores[others[0]])
+    for d in others:
+        mask &= topo.mask(core, T.cores[d])
+    eng = [e for e in topo.engines(core, T.cores[others[0]]) if mask >> e & 1]
+
+    def dst(d):
+        rid, pid = topo.addr(T.cores[d], core)
+        return DstId(rid=rid, pnc=pid)
+
+    def send(codes, plane, col, lc, lp, land, w, sem, tok):
+        need("g", tok)
+        for what in (0, 1):
+            tr = []
+            for i, d in enumerate(others):
+                a, b = col(d), land(d)
+                if what == 0:
+                    src, to = codes[:, a:a + w].bitcast(dt.uint8), lc[:, b:b + w].bitcast(dt.uint8)
+                else:
+                    src, to = plane[:, a:a + w], lp[:, b:b + w]
+                tr.append(RemoteDMATransfer(dst_ids=[dst(d)], dma_engine_mask=1 << eng[i + what], remote_sem=T.sem[sem], srcs=[src], dsts=[to]))
+            g.remote_dma_fused(tr, local_sem=T.sem.loc)
+            cnt["loc"] = cnt.get("loc", 0) + len(others)
+
+    def slot(d):
+        return 128 + W * ((r - d) % N - 1)
+
+    k_p = inc(S.dma_start(T.pst[:, 0:128], T.p[:, 0:128]), "lp", 16)
+    k_xa = inc(Y.dma_start(T.xs[:, 0:512], T.x[:, 0:512]), "lxa", 16)
+    k_xb = inc(S.dma_start(T.xs[:, 512:1024], T.x[:, 512:1024]), "lxb", 16)
+    need("y", k_xa, k_xb)
+    k_a = inc(Y.dma_start(T.as_[:], T.a[:]), "la_", 16)
+    k_w = inc(Y.dma_start(T.ws[:], T.w[:]), "lw", 16)
+    k_v = inc(Y.dma_start(T.vsb[:], T.v[:]), "lv", 16)
+
+    def iota(out, pattern, base):
+        return gc(g.iota(out, pattern, base, 0, allow_small_or_imprecise_dtypes=True))
+
+    c_pi = gc(g.iota(T.pi[:], [[0, 1]], 0, 1))
+    c_th = iota(T.th0[:], [[16, NE]], -7)
+    c_q0 = iota(T.q0[:], [[4, 36]], 0)
+    c_on = iota(T.ones[:], [[0, 256]], 1)
+    if r:
+        iota(T.sb[:, 2 * r:2 * r + 2], [[-14, 2]], 0)
+        need("g", iota(T.d0[:], [[0, 24]], 1))
+        c_d0 = iota(T.d0[:, 2 * r:2 * r + 1], [[0, 1]], 4)
+
+    m1 = v(V.memset(T.mk1[:], 0.0))
+    m2 = v(V.memset(T.zr[:], 0.0))
+    v(V.memset(T.eq[:, 0:1], 0.0))
+    v(V.memset(T.sf[:, 0:1], 0.0))
+    need("v", m1)
+    v(V.memset(T.mk1[:, 0:256:32], -2 * BIG))
+    m4 = v(V.memset(T.mk1[:, 31:256:32], BIG))
+    need("s", k_p)
+    cp = [s_(S.activation(T.pst[:, 128 * k:128 * k + 128], T.pst[:, 0:128], Act.Copy)) for k in (1, 2)]
+    if r:
+        v(V.memset(T.sb[:, 2 * r + 2:2 * r + 3], 402653184.0))
+        v(V.memset(T.sb[:, 2 * r + 3:2 * r + 4], -402653184.0))
+    need("v", c_pi)
+    v(V.tensor_scalar(T.ii[:, 0:1], T.pi[:], 15, None, Op.bitwise_and))
+    v(V.tensor_scalar(T.ii[:, 1:2], T.pi[:], 2, 3, Op.logical_shift_right, Op.bitwise_and))
+    k = v(V.tensor_scalar(T.ii[:, 2:3], T.pi[:], 3, None, Op.bitwise_and))
+    need("v", k)
+    v(V.tensor_copy(T.fi[:, 0:2], T.ii[:, 0:2]))
+    k = v(V.tensor_scalar(T.fi[:, 2:3], T.ii[:, 2:3], 28.0, None, Op.add))
+    need("v", k, c_th, c_q0)
+    v(V.tensor_scalar(T.thr[:], T.th0[:], T.fi[:, 0:1], None, Op.add))
+    k = v(V.tensor_scalar(T.q[:], T.q0[:], T.fi[:, 1:2], None, Op.add))
+    thr = T.thr
+    need("v", k)
+    if early:
+        v(V.tensor_scalar(T.t1[:], T.thr[:], 0.0, 128.0, Op.is_le, Op.mult))
+    kqm = v(V.tensor_scalar(T.qm[:], T.q[:], 3641.0, None, Op.mult))
+    v(V.tensor_scalar(T.b1[:], T.q[:], 8.0, -8.0 * early, Op.mult, Op.add))
+    if early:
+        need("v", kqm)
+        k = v(V.tensor_tensor(T.t2[:], T.thr[:], T.t1[:], Op.add))
+        need("v", k)
+        k = v(V.tensor_scalar(T.t3[:], T.t2[:], 129.0, None, Op.is_lt))
+        need("v", k)
+        v(V.tensor_tensor(T.t4[:], T.t2[:], T.t3[:], Op.mult))
+        thr = T.t4
+
+    need("v", k_p)
+    k = v(V.tensor_copy(T.pst[:, 384:512], T.pst[:, 0:128]))
+    need("v", k, cp[-1])
+    v(V.quantize_mx(T.pc[:], T.pp[:], T.pst[:]))
+    need("v", k_xa)
+    kx0 = v(V.quantize_mx(T.xc[:, 0:128], T.xp[:, 0:128], T.xs[:, 0:512]))
+    need("v", k_xb)
+    kx = v(V.quantize_mx(T.xc[:, 128:256], T.xp[:, 128:256], T.xs[:, 512:1024]))
+    need("t", kx0)
+    ks0 = t_(E.matmul_mx(T.ps0[:, 0:128], T.pc[:], T.pp[:], T.xc[:, 0:128], T.xp[:, 0:128], True, True))
+    need("t", kx)
+    ks1 = t_(E.matmul_mx(T.ps7[:, 0:128], T.pc[:], T.pp[:], T.xc[:, 128:256], T.xp[:, 128:256], True, True))
+    if early:
+        send(T.xc, T.xp, lambda d: 0, T.fc, T.fp, slot, early, "ae", kx0)
+    c_jm = iota(T.jm[:], [[0, 16], [1, 16]], 0)
+    c_hb = iota(T.hb[:, 0:4 * (N - 1) * RW], [[0, 4 * (N - 1) * RW]], 0)
+
+    need("v", m4)
+    kpm = []
+    for h, ks in ((0, ks0), (128, ks1)):
+        need("v", ks)
+        k = v(V.transpose(T.tr[:, h:h + 128], (T.ps7 if h else T.ps0)[:, 0:128]))
+        need("v", k)
+        kpm.append(v(V.tensor_tensor_scan(T.pm[:, h:h + 128], T.mk1[:, h:h + 128], T.tr[:, h:h + 128], 0.0, Op.add, Op.max)))
+    need("s", m2)
+    for bs in (range(0, 4), range(4, SB)):
+        need("s", kpm[bs[0] // 4])
+        for b in bs:
+            k = s_(S.activation(T.sgl[:, 16 * b:16 * b + 16], T.pm[:, 32 * b:32 * b + 16], Act.Sign, bias=T.pm[:, 32 * b + 15:32 * b + 16],
+                                scale=-1.0, accum_out=T.lab[:, b:b + 1]))
+        need("s", k)
+        for b in bs:
+            kbs = s_(S.activation(T.bc[:, 32 * b:32 * b + 32], T.zr[:], Act.Identity, bias=T.lab[:, b:b + 1]))
+    o = 256 - VL
+    need("v", kpm[1])
+    k = v(V.tensor_tensor(T.eq[:, 1:VL], T.pm[:, o + 1:256], T.pm[:, o:255], Op.is_equal))
+    need("v", k, c_on)
+    kls = v(V.tensor_tensor_scan(T.ls[:], T.ones[:, 0:VL], T.eq[:], 0.0, Op.add, Op.mult))
+    need("v", kls)
+    for b in range(SB, 8):
+        k = v(V.tensor_scalar(T.bc[:, 32 * b:32 * b + 32], T.zr[:], T.ls[:, 32 * b - o + 15:32 * b - o + 16], 15.0, Op.subtract, Op.add))
+    need("v", k, kbs)
+    krow = v(V.transpose(T.row[:], T.bc[:]))
+    need("v", krow)
+    kf = v(V.tensor_tensor(T.sf[:, 1:256], T.row[:, 1:256], T.row[:, 0:255], Op.not_equal))
+    v(V.tensor_scalar(T.tpk[:, 0:1], T.row[:, 255:256], 16.0, T.row[:, 0:1], Op.mult, Op.add))
+    need("v", kf)
+    kcum = v(V.tensor_tensor_scan(T.cum[:], T.ones[:], T.sf[:], 0.0, Op.mult, Op.add))
+    need("v", kcum)
+    if r < N - 1:
+        kmsg = v(V.tensor_scalar(T.msg[:, 0:1], T.tpk[:, 0:1], 256.0, T.cum[:, 255:256], Op.mult, Op.add))
+        need("g", kmsg)
+        later = list(range(r + 1, N))
+        g.remote_dma_fused([RemoteDMATransfer(dst_ids=[dst(d) for d in later], dma_engine_mask=mask, remote_sem=T.sem.inf_,
+                                              srcs=[T.msg[:, 0:1]], dsts=[T.info[:, r:r + 1]] * len(later))], local_sem=T.sem.loc)
+        cnt["loc"] = cnt.get("loc", 0) + len(eng)
+
+    kte = v(V.tensor_scalar(T.te[:], thr[:], T.cum[:, 255:256], 0.5, Op.min, Op.subtract))
+    need("s", kte)
+    for i, c in enumerate(SC):
+        kss = s_(S.activation(T.sg[:, 256 * i:256 * i + 256], T.cum[:], Act.Sign, bias=T.te[:, c:c + 1], scale=-1.0, accum_out=T.ss[:, c:c + 1]))
+
+    def compare(i):
+        return v(V.tensor_scalar(T.cm[:, 256 * i:256 * i + 256], T.cum[:], T.te[:, VC[i]:VC[i] + 1], 2.0, Op.is_lt, Op.mult))
+
+    def count(i):
+        return v(V.tensor_tensor_scan(T.cs[:, 256 * i:256 * i + 256], T.ones[:], T.cm[:, 256 * i:256 * i + 256], -256.0, Op.mult, Op.add))
+
+    need("v", kte)
+    k = v(V.tensor_scalar(T.qd[:], T.qm[:], 16, None, Op.logical_shift_right))
+    compare(0)
+    need("v", k)
+    k = v(V.tensor_scalar(T.b2[:], T.qd[:], -143.0, None, Op.mult))
+    compare(1)
+    need("v", k)
+    k = v(V.tensor_tensor(T.b3[:], T.b1[:], T.b2[:], Op.add))
+    compare(2)
+    need("v", k)
+    if early:
+        v(V.tensor_scalar(T.b5[:], T.b3[:], 0.0, 136.0, Op.is_lt, Op.mult))
+    kb4 = v(V.tensor_scalar(T.b4[:], T.b3[:], 0.0, 136.0, Op.max, Op.min))
+    k = compare(3)
+    count(0)
+    need("v", kb4)
+    b4 = T.b4
+    if early:
+        kb4 = v(V.tensor_tensor(T.b6[:], T.b4[:], T.b5[:], Op.add))
+        b4 = T.b6
+    count(1)
+    need("v", kb4)
+    v(V.tensor_scalar(T.base[:], b4[:], 4.0, T.fi[:, 2:3], Op.mult, Op.add))
+    count(2)
+    need("v", k)
+    k = count(3)
+    need("v", k)
+    k = v(V.tensor_copy(T.ss[:, VC[0]:VC[-1] + 1], T.cs[:, 255:256 * NV:256]))
+    if r:
+        v(V.tensor_copy(T.fb[:, r - 1:r], T.row[:, 0:1]))
+    need("v", k, kss)
+    for t in (2, 3, 0, 1):
+        k = v(V.tensor_scalar(T.of[:, NO * t:NO * t + NE], T.ss[:], 2.0, 512.0 + t, Op.mult, Op.add))
+        if t == 3:
+            kof = k
+    need("s", kof)
+    for t in (2, 3):
+        kcs = s_(S.activation(T.ct[:, t:64 * NE:4], T.xs[:, 0:1024].indirect(T.of[:, NO * t:NO * t + NE]), Act.Copy))
+    need("v", k)
+    for t in (0, 1):
+        kcv = v(V.tensor_copy(T.ct[:, t:64 * NE:4], T.xs[:, 0:1024].indirect(T.of[:, NO * t:NO * t + NE])))
+    need("v", c_hb)
+    kfil = v(V.quantize_mx(T.rc[:, 128:RLAND], T.rp[:, 128:RLAND], T.hb[:, 0:4 * (N - 1) * RW]))
+
+    if r:
+        need("v", c_d0, ("inf_", r * len(eng)))
+        k = v(V.tensor_copy(T.inf[:, 0:r], T.info[:, 0:r]))
+        v(V.tensor_copy(T.sb[:, r:2 * r], T.info[:, 0:r]))
+        need("v", k)
+        kla = v(V.tensor_scalar(T.la[:, 0:r], T.inf[:, 0:r], 12, None, Op.logical_shift_right))
+        if r > 1:
+            kla = v(V.tensor_scalar(T.fb[:, 0:r - 1], T.inf[:, 1:r], 8, 15, Op.logical_shift_right, Op.bitwise_and))
+        need("v", kla)
+        k = v(V.tensor_tensor(T.sb[:, 0:r], T.la[:, 0:r], T.fb[:, 0:r], Op.not_equal))
+        need("v", k)
+        k = v(V.tensor_tensor_scan(T.so[:, 0:2 * r + 4], T.d0[:, 0:2 * r + 4], T.sb[:, 0:2 * r + 4], 0.0, Op.mult, Op.add))
+        need("v", k)
+        koff = v(V.tensor_scalar(T.off[:], T.base[:], T.so[:, 2 * r:2 * r + 1], T.so[:, 2 * r + 3:2 * r + 4], Op.subtract, Op.add))
+    else:
+        koff = v(V.tensor_copy(T.off[:], T.base[:]))
+    need("s", koff, kcs, kcv)
+    kgs = s_(S.activation(T.hs[:, H0 + 2 * NB:H0 + 4 * NB], T.ct[:].indirect(T.off[:, 18:36]), Act.Copy))
+    need("v", koff, kcs, kcv)
+    kgv = v(V.tensor_copy(T.hs[:, H0:H0 + 2 * NB], T.ct[:].indirect(T.off[:, 0:18])))
+    need("v", kgs, kgv)
+    ksq = v(V.quantize_mx(T.sc[:], T.sp[:], T.hs[:, H0:H0 + 4 * NB]))
+    send(T.sc, T.sp, lambda d: W * d + early, T.fc, T.fp, lambda d: slot(d) + early, W - early, "af", ksq)
+
+    k = v(V.memset(T.hs[:, 0:H0], 0.0))
+    need("v", k)
+    i = 4 * (PAD + W * r + W)
+    kown = v(V.quantize_mx(T.fc[:, 0:128], T.fp[:, 0:128], T.hs[:, i - 512:i]))
+    need("v", k_a)
+    kaq = v(V.quantize_mx(T.ac[:], T.apl[:], T.as_[:]))
+    need("v", k_w)
+    kwq = v(V.quantize_mx(T.wc[:], T.wp[:], T.ws[:]))
+    need("v", k_v)
+    kvq = v(V.quantize_mx(T.vc[:], T.vp[:], T.vsb[:]))
+    need("t", kwq)
+    kw = t_(E.matmul_mx(T.ps5[:, 0:256], T.wc[:], T.wp[:], T.xc[:], T.xp[:], True, True))
+    need("s", kw)
+    kwy = s_(S.activation(T.wy[:], T.ps5[:, 0:256], Act.Copy))
+    klb0 = s_(S.activation(T.lbt[0:1, 0:256], T.row[0:1, :], Act.Copy))
+    need("v", c_jm)
+    k = v(V.tensor_scalar(T.m16[:], T.jm[:], T.fi[:, 0:1], None, Op.is_equal))
+    krm = v(V.memset(T.rm[:], 1.0))
+    need("v", k, krm)
+    krm = v(V.memset(T.rm[:, 0:256:16], 0.0))
+    kc0 = v(V.tensor_tensor(T.cw0[:], T.cum[:], T.m16[:], Op.mult))
+    need("v", krm, kc0)
+    kcw = v(V.tensor_tensor_scan(T.cw1[:], T.rm[:], T.cw0[:], 0.0, Op.mult, Op.add))
+
+    need("t", kaq, kown, ("af", 2 * len(others)), ("ae", 0 if early else 2))
+    ps = [T.ps1, T.ps2, T.ps3, T.ps4]
+    km = [t_(E.matmul_mx(ps[i][:, 0:NB], T.ac[:, 128 * i:128 * i + 128], T.apl[:, 128 * i:128 * i + 128],
+                         T.fc[:, 128 - W:LAND], T.fp[:, 128 - W:LAND], True, True)) for i in range(4)]
+    for i in (0, 2):
+        need("v", km[i])
+        kh = v(V.tensor_scalar(T.hb[:, H0 + i:H0 + 4 * NB:4], ps[i][:, 0:NB], 0.0, 0.05, Op.max, Op.mult))
+    need("s", kfil)
+    for i in (1, 3):
+        need("s", km[i])
+        khs = s_(S.activation(T.hb[:, H0 + i:H0 + 4 * NB:4], ps[i][:, 0:NB], Act.Relu, scale=0.05))
+    need("v", kh, khs)
+    khq = v(V.quantize_mx(T.hc[:], T.hp[:], T.hb[:, H0:H0 + 4 * NB]))
+    send(T.hc, T.hp, lambda d: W * ((d - r) % N) - 1, T.rc, T.rp, lambda d: 128 + RW * ((r - d) % N - 1), W + 1, "ar", khq)
+    k = v(V.tensor_copy(T.hb[:, H0 - 4:H0], T.hb[:, H0 + 4 * NB - 4:H0 + 4 * NB]))
+    need("v", k)
+    i = 4 * (PAD - 1 + RW)
+    krq = v(V.quantize_mx(T.rc[:, 0:128], T.rp[:, 0:128], T.hb[:, i - 512:i]))
+
+    cw = T.cw1[:, 15:256:16]
+    if r:
+        v(V.tensor_scalar(T.bt[:, 0:1], T.so[:, 2 * r:2 * r + 1], T.so[:, 2 * r + 3:2 * r + 4], 0.25, Op.subtract, Op.mult))
+        kbt = v(V.tensor_scalar(T.bt[:, 1:2], T.sb[:, r - 1:r], -1.0, 1.0 + early, Op.mult, Op.add))
+    else:
+        kbt = v(V.memset(T.bt[:, 0:2], 0.0))
+    need("v", kbt, kcw)
+    v(V.tensor_scalar(T.gi[:], cw, T.bt[:, 0:1], None, Op.add))
+    kgr = v(V.tensor_scalar(T.gr[:], cw, T.bt[:, 0:1], float(N - r), Op.add, Op.add))
+    v(V.tensor_scalar(T.z[:], cw, 0.0, T.bt[:, 1:2], Op.is_equal, Op.mult))
+    need("v", kgr)
+    v(V.tensor_scalar(T.h1[:], T.gi[:], 3, 15 if early else 31, Op.logical_shift_right, Op.bitwise_and))
+    k = v(V.tensor_scalar(T.d1[:], T.gr[:], 7, None, Op.bitwise_and))
+    need("v", k)
+    k = v(V.tensor_scalar(T.u[:], T.d1[:], float(RW), 1.0 + early, Op.mult, Op.add))
+    need("v", k)
+    k = v(V.tensor_tensor(T.u2[:], T.u[:], T.h1[:], Op.add))
+    need("v", k)
+    k = v(V.tensor_tensor(T.u3[:], T.u2[:], T.z[:], Op.subtract))
+    need("v", k)
+    kpos = v(V.tensor_copy(T.pos[:], T.u3[:]))
+    if r:
+        k = v(V.tensor_scalar(T.ni[:, 0:r], T.inf[:, 0:r], 255, None, Op.bitwise_and))
+        v(V.tensor_copy(T.nf[:, r:2 * r], T.sb[:, 0:r]))
+        need("v", k)
+        k = v(V.tensor_copy(T.nf[:, 0:r], T.ni[:, 0:r]))
+        need("v", k)
+        k = v(V.tensor_reduce(T.bt[:, 2:3], T.nf[:, 0:2 * r], AxisListType.X, Op.add))
+        need("v", k)
+        klb = v(V.tensor_scalar(T.lbt[0:1, 256:512], T.cum[0:1, :], T.bt[0:1, 2:3], None, Op.add))
+    else:
+        klb = v(V.tensor_copy(T.lbt[0:1, 256:512], T.cum[0:1, :]))
+    need("y", klb, klb0)
+    kslb = inc(Y.dma_start(T.lb[:], T.lbt[0:1, :]), "slb", 16)
+
+    need("t", kvq, krq, ("ar", 2 * len(others)))
+    kvm = t_(E.matmul_mx(T.ps6[:, 0:NR], T.vc[:], T.vp[:], T.rc[:, 128 - RW:RLAND], T.rp[:, 128 - RW:RLAND], True, True))
+    need("v", kvm)
+    k = v(V.tensor_copy(T.vw[:], T.ps6[:, 0:NR]))
+    need("v", k, kwy, kpos)
+    ky0 = v(V.tensor_tensor(T.yt[:, 0:128], T.vw[:].indirect(T.pos[:, 0:8]), T.wy[:, 0:128], Op.add))
+    ky1 = v(V.tensor_tensor(T.yt[:, 128:256], T.vw[:].indirect(T.pos[:, 8:16]), T.wy[:, 128:256], Op.add))
+    need("y", ky0)
+    ks0 = inc(Y.dma_start(T.y[:, 0:128], T.yt[:, 0:128]), "sy0", 16)
+    need("s", ky1)
+    ks1 = inc(S.dma_start(T.y[:, 128:256], T.yt[:, 128:256]), "sy1", 16)
+    need("y", kslb, ks0)
+    need("s", ks1)
+    need("y", k_a, k_w, k_v)
+    need("g", ("loc", cnt["loc"]))
+    for sem in ("gc", "v", "s", "t"):
+        need("g", (sem, cnt[sem]))

@@ -3,56 +3,109 @@ from concourse.mybir import dt, AluOpType as Op, AxisListType, ActivationFunctio
 
 N, TC = 8, 256
 W = 18
-RW = 20
+RW = W + 2
 NB, NR = N * W, N * RW
-PAD = 112
-H0 = 4 * PAD
-LAND, RLAND = 128 + (N - 1) * W, 128 + (N - 1) * RW
+FL, FM = 128, 272
 NE = 9
 NO = NE + 1
-SC = [0, 1, 2, 3, 4]
-VC = [5, 6, 7, 8]
-NV = len(VC)
+VC, SC = [0, 1, 2, 3], [4, 5, 6, 7, 8]
+J0 = 48
 BIG = 1e29
-SB = 5
-VL = 256 - 32 * SB
+RND = 1.5 * 2 ** 23
+NEAR = 3
+W1 = RW * (NEAR + 1)
+HL = 256
+RELAY = [list(range(1, N)), list(range(1, N - NEAR)), list(range(1, NEAR + 1))]
+DIRECT = [[b for b in range(1, N) if b not in bs] for bs in RELAY]
 
 SCRATCH = {}
 for _n, _w, _t in (
-        ("xs", 1024, "bfloat16"), ("pst", 512, "bfloat16"), ("as_", 2048, "bfloat16"), ("ws", 512, "bfloat16"), ("vsb", 512, "bfloat16"),
-        ("tr", 256, "float32"), ("pm", 256, "float32"), ("mk1", 256, "float32"), ("eq", VL, "bfloat16"), ("ls", VL, "bfloat16"),
-        ("zr", 32, "bfloat16"), ("lab", 8, "float32"), ("sgl", 128, "bfloat16"), ("bc", 256, "bfloat16"), ("row", 256, "bfloat16"),
-        ("sf", 256, "bfloat16"), ("cum", 256, "bfloat16"), ("ones", 256, "bfloat16"), ("tpk", 8, "float32"), ("msg", 2, "uint16"),
-        ("pi", 1, "int32"), ("ii", 4, "int32"), ("fi", 4, "float32"), ("th0", NE, "float32"), ("thr", NE, "float32"), ("te", NE, "float32"),
-        ("t1", NE, "float32"), ("t2", NE, "float32"), ("t3", NE, "float32"), ("t4", NE, "float32"),
-        ("ss", NE, "float32"), ("sg", 256 * len(SC), "bfloat16"), ("cm", 256 * NV, "bfloat16"), ("cs", 256 * NV, "bfloat16"), ("of", 4 * NO, "uint16"),
-        ("ct", 64 * NE, "bfloat16"), ("q0", 36, "float32"), ("q", 36, "float32"), ("qm", 36, "int32"), ("qd", 36, "int32"), ("b1", 36, "float32"),
-        ("b2", 36, "float32"), ("b3", 36, "float32"), ("b4", 36, "float32"), ("b5", 36, "float32"), ("b6", 36, "float32"), ("base", 36, "float32"),
-        ("off", 36, "uint16"), ("info", 8, "uint16"), ("inf", 8, "int32"),
+        ("xs", 1040, "bfloat16"), ("pst", 576, "bfloat16"), ("as_", 2048, "bfloat16"), ("ws", 512, "bfloat16"), ("vsb", 512, "bfloat16"),
+        ("tr", 128, "float32"), ("pm", 132, "float32"), ("mk", 128, "float32"), ("nf", 128, "bfloat16"), ("dd", 144, "bfloat16"),
+        ("ta", 288, "bfloat16"), ("mh", 128, "bfloat16"), ("bc", 256, "bfloat16"), ("row", 256, "bfloat16"),
+        ("df", 256, "bfloat16"), ("sf", 256, "bfloat16"), ("cum", 256, "bfloat16"), ("ones", 256, "bfloat16"),
+        ("tp", 2, "float32"), ("msg", 2, "uint16"),
+        ("tb", 160, "bfloat16"), ("fi", 160, "bfloat16"), ("th1", NE, "float32"), ("th0", NE, "float32"), ("thr", NE, "float32"), ("te", 1, "float32"),
+        ("ss", NE, "float32"), ("sg", 256 * len(SC), "bfloat16"), ("cm", 256 * len(VC), "bfloat16"), ("cs", 256 * len(VC), "bfloat16"),
+        ("of", 4 * NO, "uint16"), ("ct", 64 * NE, "bfloat16"), ("q0", 36, "float32"), ("q", 36, "float32"), ("qm", 36, "float32"),
+        ("qd", 36, "float32"), ("qe", 36, "float32"), ("b1", 36, "float32"), ("b2", 36, "float32"), ("b3", 36, "float32"), ("b4", 36, "float32"),
+        ("b5", 36, "float32"), ("base", 36, "float32"), ("off", 36, "uint16"), ("info", 8, "uint16"), ("inf", 8, "int32"),
         ("la", 8, "int32"), ("fb", 8, "int32"), ("sb", 24, "float32"), ("d0", 24, "float32"), ("so", 24, "float32"),
-        ("hs", 4 * (PAD + NB), "bfloat16"), ("hb", 4 * (PAD + NB), "bfloat16"),
-        ("jm", 256, "float32"), ("m16", 256, "bfloat16"), ("rm", 256, "bfloat16"), ("cw0", 256, "bfloat16"), ("cw1", 256, "bfloat16"),
+        ("hs", 4 * NB, "bfloat16"), ("hb", 4 * NR, "bfloat16"),
+        ("jm", 256, "bfloat16"), ("mq", 256, "bfloat16"), ("cw1", 256, "bfloat16"),
         ("bt", 4, "float32"), ("gi", 16, "int32"), ("gr", 16, "int32"), ("h1", 16, "int32"), ("d1", 16, "int32"), ("z", 16, "float32"),
-        ("u", 16, "float32"), ("u2", 16, "float32"), ("u3", 16, "float32"), ("pos", 16, "uint16"), ("ni", 8, "int32"), ("nf", 16, "float32"),
-        ("lbt", 512, "float32"), ("wy", 256, "float32"), ("vw", NR, "float32"), ("yt", 256, "float32")):
+        ("u", 16, "float32"), ("u2", 16, "float32"), ("pos", 16, "uint16"), ("u3", 16, "float32"), ("ni", 8, "int32"), ("nn", 16, "float32"),
+        ("lbt", 512, "float32"), ("wy", 128, "float32"), ("vw", NR, "float32"), ("vg", 128, "float32"), ("yt", 256, "float32")):
     SCRATCH[_n] = ("sbuf", [128, _w], _t)
-for _n, _m, _w in (("pc", "pp", 128), ("xc", "xp", 256), ("ac", "apl", 512), ("wc", "wp", 128), ("vc", "vp", 128),
-                   ("sc", "sp", NB), ("fc", "fp", LAND), ("hc", "hp", NB), ("rc", "rp", RLAND)):
+for _n, _m, _w in (("pc", "pp", 144), ("xc", "xp", 256), ("ac", "apl", 512), ("wc", "wp", 128), ("vc", "vp", 128),
+                   ("fc", "fp", FM + 128), ("hc", "hp", HL + NR - RW)):
     SCRATCH[_n] = ("sbuf", [128, _w], "float8_e4m3fn_x4")
     SCRATCH[_m] = ("sbuf", [128, _w], "uint8")
-for _i in range(8):
+for _i in range(7):
     SCRATCH["ps%d" % _i] = ("psum", [128, 512], "float32")
-SEMAPHORES = ["v", "s", "t", "gc", "lp", "lxa", "lxb", "la_", "lw", "lv", "inf_", "ae", "af", "ar", "loc", "sy0", "sy1", "slb"]
+SEMAPHORES = ["v", "s", "t", "gc", "lp", "lxa", "lxb", "la_", "lw", "lv", "inf_", "af", "ar", "loc", "sy0", "sy1", "slb",
+              "l1", "r0", "r1", "r2", "ag", "ae"]
+
+
+def helpers(core, T, topo):
+    return [c for c in topo.cores_of(core) if topo.die(c) != topo.die(core)
+            and all(topo.may_write(c, d) for d in T.cores if d != core)][:2]
+
+
+def steps(T):
+    xs, fs, hs = (T.xc, T.xp), (T.fc, T.fp), (T.hc, T.hp)
+    return ((xs, lambda b: 0, fs, lambda b: FL + RW * (N - b - 1), RW - W, "ae", "ae"),
+            (fs, lambda b: FM + W * (b - 1), fs, lambda b: FL + RW * (N - b) - W, W, "af", "ag"),
+            (hs, lambda b: RW * b - 2 + (HL - NR) * (b > NEAR), hs, lambda b: HL + RW * (N - b - 1), RW, "ar", "ar"))
+
+
+WHOLE = [(False, False), (True, False), (True, True)]
+
+
+def view(bufs, what, a, w):
+    return bufs[1][:, a:a + w] if what else bufs[0][:, a:a + w].bitcast(dt.uint8)
+
+
+def shares(eng, n, turn):
+    size = [1] * n
+    while sum(size) + min(size) <= len(eng):
+        size[size.index(min(size))] *= 2
+    size = size[::-1] if turn else size
+    out, at = [], 0
+    for k in size:
+        out.append(sum(1 << e for e in eng[at:at + k]))
+        at += k
+    return out, size
+
+
+def outward(T, topo, core, r, j, what, bs, which):
+    src, at, to, land, w = steps(T)[j][:5]
+    tr = []
+    for b, m in zip(bs, shares(topo.engines(core, T.cores[(r + 1) % N]), len(bs), what)[0]):
+        rid, pid = topo.addr(T.cores[(r + b) % N], core)
+        tr.append(RemoteDMATransfer(dst_ids=[DstId(rid=rid, pnc=pid)], dma_engine_mask=m, remote_sem=T.sem[steps(T)[j][5 + which]],
+                                    srcs=[view(src, what, at(b), w)], dsts=[view(to, what, land(b), w)]))
+    return tr
+
+
+def helper_program(g, core, T, topo, r, what):
+    out = len(topo.engines(core, T.cores[(r + 1) % N]))
+    for j in range(3):
+        g.wait_ge(T.sem["r%d" % j], len(topo.engines(T.cores[r], core)) - (0 if WHOLE[j][what] else out))
+        g.remote_dma_fused(outward(T, topo, core, r, j, what, RELAY[j], 1), local_sem=T.sem.loc)
+    g.wait_ge(T.sem.loc, 3 * out)
 
 
 def rank_program(g, core, T, topo):
     r = T.rank_of(core)
     if r is None:
+        for i, c in enumerate(T.cores):
+            if core in topo.cores_of(c) and core in helpers(c, T, topo):
+                helper_program(g, core, T, topo, i, helpers(c, T, topo).index(core))
         return
     V, S, E, Y = g.vector, g.scalar, g.tensor, g.sync
     queues = {"v": V, "s": S, "t": E, "y": Y, "g": g}
     cnt, seen = {}, {}
-    early = 2 if r == N - 1 else 0
 
     def inc(ins, sem, n=1):
         ins.then_inc(T.sem[sem], n)
@@ -73,201 +126,185 @@ def rank_program(g, core, T, topo):
     def t_(ins): return inc(ins, "t")
     def gc(ins): return inc(ins, "gc")
 
-    others = [(r + k) % N for k in range(1, N)]
-    mask = topo.mask(core, T.cores[others[0]])
-    for d in others:
-        mask &= topo.mask(core, T.cores[d])
-    eng = [e for e in topo.engines(core, T.cores[others[0]]) if mask >> e & 1]
+    eng = topo.engines(core, T.cores[(r + 1) % N])
+    hlp = helpers(core, T, topo)
 
-    def dst(d):
-        rid, pid = topo.addr(T.cores[d], core)
+    def dst(c):
+        rid, pid = topo.addr(c, core)
         return DstId(rid=rid, pnc=pid)
 
-    def send(codes, plane, col, lc, lp, land, w, sem, tok):
+    def inward(j, what):
+        src, at, w = steps(T)[j][0], steps(T)[j][1], steps(T)[j][4]
+        run = view(src, what, at(1), w * (len(RELAY[j]) if j else 1 + 3 * what))
+        use = [e for e in topo.engines(core, hlp[what]) if WHOLE[j][what] or (e in eng) == (j + what == 0)]
+        cnt["loc"] = cnt.get("loc", 0) + len(use)
+        return [RemoteDMATransfer(dst_ids=[dst(hlp[what])], dma_engine_mask=sum(1 << e for e in use), remote_sem=T.sem["r%d" % j],
+                                  srcs=[run], dsts=[run])]
+
+    def direct(j, what):
+        cnt["loc"] = cnt.get("loc", 0) + len(eng)
+        return outward(T, topo, core, r, j, what, DIRECT[j], 0)
+
+    def send(tok, *calls):
         need("g", tok)
-        for what in (0, 1):
-            tr = []
-            for i, d in enumerate(others):
-                a, b = col(d), land(d)
-                if what == 0:
-                    src, to = codes[:, a:a + w].bitcast(dt.uint8), lc[:, b:b + w].bitcast(dt.uint8)
-                else:
-                    src, to = plane[:, a:a + w], lp[:, b:b + w]
-                tr.append(RemoteDMATransfer(dst_ids=[dst(d)], dma_engine_mask=1 << eng[i + what], remote_sem=T.sem[sem], srcs=[src], dsts=[to]))
+        for tr in calls:
             g.remote_dma_fused(tr, local_sem=T.sem.loc)
-            cnt["loc"] = cnt.get("loc", 0) + len(others)
 
-    def slot(d):
-        return 128 + W * ((r - d) % N - 1)
-
-    k_p = inc(S.dma_start(T.pst[:, 0:128], T.p[:, 0:128]), "lp", 16)
+    k_p = inc(S.dma_start(T.pst[:, 64:192], T.p[:, 0:128]), "lp", 16)
     k_xa = inc(Y.dma_start(T.xs[:, 0:512], T.x[:, 0:512]), "lxa", 16)
     k_xb = inc(S.dma_start(T.xs[:, 512:1024], T.x[:, 512:1024]), "lxb", 16)
     need("y", k_xa, k_xb)
     k_a = inc(Y.dma_start(T.as_[:], T.a[:]), "la_", 16)
-    k_w = inc(Y.dma_start(T.ws[:], T.w[:]), "lw", 16)
-    k_v = inc(Y.dma_start(T.vsb[:], T.v[:]), "lv", 16)
 
     def iota(out, pattern, base):
         return gc(g.iota(out, pattern, base, 0, allow_small_or_imprecise_dtypes=True))
 
-    c_pi = gc(g.iota(T.pi[:], [[0, 1]], 0, 1))
-    c_th = iota(T.th0[:], [[16, NE]], -7)
+    for i, (pattern, base) in enumerate((([[0, 2], [1, 16]], 0), ([[0, 2], [1, 4], [0, 4]], 0), ([[0, 8], [1, 4]], 28),
+                                         ([[0, 2], [128, 2], [0, 8]], 0), ([[0, 2], [-120, 2], [1, 8]], 241))):
+        c_tb = iota(T.tb[:, 32 * i:32 * i + 32], pattern, base)
     c_q0 = iota(T.q0[:], [[4, 36]], 0)
-    c_on = iota(T.ones[:], [[0, 256]], 1)
-    if r:
-        iota(T.sb[:, 2 * r:2 * r + 2], [[-14, 2]], 0)
-        need("g", iota(T.d0[:], [[0, 24]], 1))
-        c_d0 = iota(T.d0[:, 2 * r:2 * r + 1], [[0, 1]], 4)
+    c_th = iota(T.th0[:], [[16, NE]], -15)
+    c_ta = iota(T.ta[:, 256:288], [[0, 32]], 0)
+    Q, Q4, T28, UP, TOP = (T.fi[:, 32 * i:32 * i + 1] for i in range(5))
 
-    m1 = v(V.memset(T.mk1[:], 0.0))
-    m2 = v(V.memset(T.zr[:], 0.0))
-    v(V.memset(T.eq[:, 0:1], 0.0))
-    v(V.memset(T.sf[:, 0:1], 0.0))
+    kz = v(V.memset(T.pst[:, 0:64], 0.0))
+    v(V.memset(T.mk[:], 0.0))
+    v(V.memset(T.dd[:], 1.0))
+    m1 = v(V.memset(T.mh[:], 0.0))
+    v(V.memset(T.pm[:, 0:1], -BIG))
     need("v", m1)
-    v(V.memset(T.mk1[:, 0:256:32], -2 * BIG))
-    m4 = v(V.memset(T.mk1[:, 31:256:32], BIG))
+    v(V.memset(T.dd[:, 15:144:32], 18.0))
+    v(V.memset(T.mh[:, 0:128:32], -128.0))
+    m4 = v(V.memset(T.mk[:, 15:128:16], -BIG))
     need("s", k_p)
-    cp = [s_(S.activation(T.pst[:, 128 * k:128 * k + 128], T.pst[:, 0:128], Act.Copy)) for k in (1, 2)]
-    if r:
-        v(V.memset(T.sb[:, 2 * r + 2:2 * r + 3], 402653184.0))
-        v(V.memset(T.sb[:, 2 * r + 3:2 * r + 4], -402653184.0))
-    need("v", c_pi)
-    v(V.tensor_scalar(T.ii[:, 0:1], T.pi[:], 15, None, Op.bitwise_and))
-    v(V.tensor_scalar(T.ii[:, 1:2], T.pi[:], 2, 3, Op.logical_shift_right, Op.bitwise_and))
-    k = v(V.tensor_scalar(T.ii[:, 2:3], T.pi[:], 3, None, Op.bitwise_and))
-    need("v", k)
-    v(V.tensor_copy(T.fi[:, 0:2], T.ii[:, 0:2]))
-    k = v(V.tensor_scalar(T.fi[:, 2:3], T.ii[:, 2:3], 28.0, None, Op.add))
-    need("v", k, c_th, c_q0)
-    v(V.tensor_scalar(T.thr[:], T.th0[:], T.fi[:, 0:1], None, Op.add))
-    k = v(V.tensor_scalar(T.q[:], T.q0[:], T.fi[:, 1:2], None, Op.add))
-    thr = T.thr
-    need("v", k)
-    if early:
-        v(V.tensor_scalar(T.t1[:], T.thr[:], 0.0, 128.0, Op.is_le, Op.mult))
-    kqm = v(V.tensor_scalar(T.qm[:], T.q[:], 3641.0, None, Op.mult))
-    v(V.tensor_scalar(T.b1[:], T.q[:], 8.0, -8.0 * early, Op.mult, Op.add))
-    if early:
-        need("v", kqm)
-        k = v(V.tensor_tensor(T.t2[:], T.thr[:], T.t1[:], Op.add))
-        need("v", k)
-        k = v(V.tensor_scalar(T.t3[:], T.t2[:], 129.0, None, Op.is_lt))
-        need("v", k)
-        v(V.tensor_tensor(T.t4[:], T.t2[:], T.t3[:], Op.mult))
-        thr = T.t4
+    cp = [s_(S.activation(T.pst[:, 64 + 128 * k:192 + 128 * k], T.pst[:, 64:192], Act.Copy)) for k in (1,)]
+    need("v", c_tb)
+    k = v(V.transpose(T.fi[:], T.tb[:]))
+    need("s", k, c_q0)
+    ks_ = s_(S.activation(T.q[:], T.q0[:], Act.Identity, bias=Q4))
+    need("s", ks_)
+    s_(S.activation(T.b1[:], T.q[:], Act.Copy, bias=9.0, scale=8.0))
+    for out, in_, bias, scale in ((T.qm, T.q, -0.47, 1.0 / W), (T.qd, T.qm, RND, 1.0), (T.qe, T.qd, -RND, 1.0), (T.b2, T.qe, 0.0, 1.0 - 8 * W)):
+        need("s", ks_)
+        ks_ = s_(S.activation(out[:], in_[:], Act.Copy, bias=bias, scale=scale))
+    need("s", c_th)
+    k = s_(S.activation(T.th1[:], T.th0[:], Act.Identity, bias=Q))
+    need("s", k)
+    kthr = s_(S.activation(T.thr[:], T.th1[:], Act.Copy, bias=-0.5))
 
     need("v", k_p)
-    k = v(V.tensor_copy(T.pst[:, 384:512], T.pst[:, 0:128]))
-    need("v", k, cp[-1])
+    v(V.tensor_copy(T.pst[:, 320:448], T.pst[:, 64:192]))
+    k = v(V.tensor_copy(T.pst[:, 448:576], T.pst[:, 64:192]))
+    need("v", k, cp[-1], kz)
     v(V.quantize_mx(T.pc[:], T.pp[:], T.pst[:]))
     need("v", k_xa)
     kx0 = v(V.quantize_mx(T.xc[:, 0:128], T.xp[:, 0:128], T.xs[:, 0:512]))
     need("v", k_xb)
     kx = v(V.quantize_mx(T.xc[:, 128:256], T.xp[:, 128:256], T.xs[:, 512:1024]))
     need("t", kx0)
-    ks0 = t_(E.matmul_mx(T.ps0[:, 0:128], T.pc[:], T.pp[:], T.xc[:, 0:128], T.xp[:, 0:128], True, True))
+    E.matmul_mx(T.ps0[:, 0:128], T.pc[:, 16:144], T.pp[:, 16:144], T.xc[:, 0:128], T.xp[:, 0:128], True, False)
     need("t", kx)
-    ks1 = t_(E.matmul_mx(T.ps7[:, 0:128], T.pc[:], T.pp[:], T.xc[:, 128:256], T.xp[:, 128:256], True, True))
-    if early:
-        send(T.xc, T.xp, lambda d: 0, T.fc, T.fp, slot, early, "ae", kx0)
-    c_jm = iota(T.jm[:], [[0, 16], [1, 16]], 0)
-    c_hb = iota(T.hb[:, 0:4 * (N - 1) * RW], [[0, 4 * (N - 1) * RW]], 0)
+    ks = t_(E.matmul_mx(T.ps0[:, 0:128], T.pc[:, 0:128], T.pp[:, 0:128], T.xc[:, 128:256], T.xp[:, 128:256], False, True))
+    send(kx0, inward(0, 0) + inward(0, 1))
+    v(V.memset(T.ones[:], 1.0))
+    v(V.memset(T.df[:, 0:1], 0.0))
 
-    need("v", m4)
-    kpm = []
-    for h, ks in ((0, ks0), (128, ks1)):
-        need("v", ks)
-        k = v(V.transpose(T.tr[:, h:h + 128], (T.ps7 if h else T.ps0)[:, 0:128]))
-        need("v", k)
-        kpm.append(v(V.tensor_tensor_scan(T.pm[:, h:h + 128], T.mk1[:, h:h + 128], T.tr[:, h:h + 128], 0.0, Op.add, Op.max)))
-    need("s", m2)
-    for bs in (range(0, 4), range(4, SB)):
-        need("s", kpm[bs[0] // 4])
-        for b in bs:
-            k = s_(S.activation(T.sgl[:, 16 * b:16 * b + 16], T.pm[:, 32 * b:32 * b + 16], Act.Sign, bias=T.pm[:, 32 * b + 15:32 * b + 16],
-                                scale=-1.0, accum_out=T.lab[:, b:b + 1]))
-        need("s", k)
-        for b in bs:
-            kbs = s_(S.activation(T.bc[:, 32 * b:32 * b + 32], T.zr[:], Act.Identity, bias=T.lab[:, b:b + 1]))
-    o = 256 - VL
-    need("v", kpm[1])
-    k = v(V.tensor_tensor(T.eq[:, 1:VL], T.pm[:, o + 1:256], T.pm[:, o:255], Op.is_equal))
-    need("v", k, c_on)
-    kls = v(V.tensor_tensor_scan(T.ls[:], T.ones[:, 0:VL], T.eq[:], 0.0, Op.add, Op.mult))
-    need("v", kls)
-    for b in range(SB, 8):
-        k = v(V.tensor_scalar(T.bc[:, 32 * b:32 * b + 32], T.zr[:], T.ls[:, 32 * b - o + 15:32 * b - o + 16], 15.0, Op.subtract, Op.add))
-    need("v", k, kbs)
+    need("v", ks, m4)
+    k = v(V.transpose(T.tr[:], T.ps0[:, 0:128]))
+    need("v", ks_)
+    kb = v(V.tensor_tensor(T.b3[:], T.b1[:], T.b2[:], Op.add))
+    need("v", k)
+    k = v(V.tensor_tensor_scan(T.pm[:, 1:129], T.tr[:], T.mk[:], -BIG, Op.max, Op.add))
+    need("v", kb)
+    kb = v(V.tensor_scalar(T.b4[:], T.b3[:], 137.0, None, Op.is_lt))
+    need("v", k)
+    k = v(V.tensor_tensor(T.nf[:], T.pm[:, 0:128], T.tr[:], Op.is_ge))
+    need("v", kb)
+    kb5 = v(V.tensor_tensor(T.b5[:], T.b3[:], T.b4[:], Op.mult))
+    need("v", k, c_ta)
+    v(V.tensor_tensor_scan(T.ta[:, 0:128], T.nf[:], T.dd[:, 0:128], 0.0, Op.mult, Op.add))
+    k = v(V.tensor_tensor_scan(T.ta[:, 128:256], T.nf[:], T.dd[:, 16:144], 0.0, Op.mult, Op.add))
+    if r:
+        v(V.memset(T.sb[:, 2 * r + 2:2 * r + 3], 402653184.0))
+    need("v", k)
+    v(V.tensor_tensor_scan(T.bc[:, 0:128], T.mh[:], T.ta[:, 15:143], 0.0, Op.add, Op.max))
+    k = v(V.tensor_tensor_scan(T.bc[:, 128:256], T.mh[:], T.ta[:, 159:287], 0.0, Op.add, Op.max))
+    if r:
+        v(V.memset(T.sb[:, 2 * r + 3:2 * r + 4], -402653184.0))
+    need("v", k)
     krow = v(V.transpose(T.row[:], T.bc[:]))
     need("v", krow)
-    kf = v(V.tensor_tensor(T.sf[:, 1:256], T.row[:, 1:256], T.row[:, 0:255], Op.not_equal))
-    v(V.tensor_scalar(T.tpk[:, 0:1], T.row[:, 255:256], 16.0, T.row[:, 0:1], Op.mult, Op.add))
-    need("v", kf)
+    k = v(V.tensor_tensor_scan(T.df[:, 1:256], T.row[:, 1:256], T.row[:, 0:255], 0.0, Op.max, Op.subtract))
+    if r:
+        v(V.tensor_scalar(T.fb[:, r - 1:r], T.row[:, 0:1], -18.0, None, Op.add))
+    need("s", kb5)
+    kbase = s_(S.activation(T.base[:], T.b5[:], Act.Identity, bias=T28, scale=4.0))
+    need("s", krow)
+    k1 = s_(S.activation(T.tp[:, 0:1], T.row[:, 0:1], Act.Copy, bias=-18.0 * 4352, scale=256.0))
+    need("s", k1)
+    ktp = s_(S.activation(T.tp[:, 1:2], T.row[:, 255:256], Act.Identity, bias=T.tp[:, 0:1], scale=4096.0))
+    need("v", k)
+    k = v(V.tensor_scalar(T.sf[:], T.df[:], 0.0, None, Op.not_equal))
+    need("v", k)
     kcum = v(V.tensor_tensor_scan(T.cum[:], T.ones[:], T.sf[:], 0.0, Op.mult, Op.add))
     need("v", kcum)
     if r < N - 1:
-        kmsg = v(V.tensor_scalar(T.msg[:, 0:1], T.tpk[:, 0:1], 256.0, T.cum[:, 255:256], Op.mult, Op.add))
+        need("v", ktp)
+        kmsg = v(V.tensor_scalar(T.msg[:, 0:1], T.cum[:, 255:256], T.tp[:, 1:2], None, Op.add))
         need("g", kmsg)
-        later = list(range(r + 1, N))
-        g.remote_dma_fused([RemoteDMATransfer(dst_ids=[dst(d) for d in later], dma_engine_mask=mask, remote_sem=T.sem.inf_,
-                                              srcs=[T.msg[:, 0:1]], dsts=[T.info[:, r:r + 1]] * len(later))], local_sem=T.sem.loc)
-        cnt["loc"] = cnt.get("loc", 0) + len(eng)
-
-    kte = v(V.tensor_scalar(T.te[:], thr[:], T.cum[:, 255:256], 0.5, Op.min, Op.subtract))
-    need("s", kte)
-    for i, c in enumerate(SC):
-        kss = s_(S.activation(T.sg[:, 256 * i:256 * i + 256], T.cum[:], Act.Sign, bias=T.te[:, c:c + 1], scale=-1.0, accum_out=T.ss[:, c:c + 1]))
-
-    def compare(i):
-        return v(V.tensor_scalar(T.cm[:, 256 * i:256 * i + 256], T.cum[:], T.te[:, VC[i]:VC[i] + 1], 2.0, Op.is_lt, Op.mult))
-
-    def count(i):
-        return v(V.tensor_tensor_scan(T.cs[:, 256 * i:256 * i + 256], T.ones[:], T.cm[:, 256 * i:256 * i + 256], -256.0, Op.mult, Op.add))
-
-    need("v", kte)
-    k = v(V.tensor_scalar(T.qd[:], T.qm[:], 16, None, Op.logical_shift_right))
-    compare(0)
-    need("v", k)
-    k = v(V.tensor_scalar(T.b2[:], T.qd[:], -143.0, None, Op.mult))
-    compare(1)
-    need("v", k)
-    k = v(V.tensor_tensor(T.b3[:], T.b1[:], T.b2[:], Op.add))
-    compare(2)
-    need("v", k)
-    if early:
-        v(V.tensor_scalar(T.b5[:], T.b3[:], 0.0, 136.0, Op.is_lt, Op.mult))
-    kb4 = v(V.tensor_scalar(T.b4[:], T.b3[:], 0.0, 136.0, Op.max, Op.min))
-    k = compare(3)
-    count(0)
-    need("v", kb4)
-    b4 = T.b4
-    if early:
-        kb4 = v(V.tensor_tensor(T.b6[:], T.b4[:], T.b5[:], Op.add))
-        b4 = T.b6
-    count(1)
-    need("v", kb4)
-    v(V.tensor_scalar(T.base[:], b4[:], 4.0, T.fi[:, 2:3], Op.mult, Op.add))
-    count(2)
-    need("v", k)
-    k = count(3)
-    need("v", k)
-    k = v(V.tensor_copy(T.ss[:, VC[0]:VC[-1] + 1], T.cs[:, 255:256 * NV:256]))
+        later = list(range(N - 1, r, -1))
+        g.remote_dma_fused([RemoteDMATransfer(dst_ids=[dst(T.cores[d]) for d in later], dma_engine_mask=sum(1 << e for e in eng),
+                                              remote_sem=T.sem.inf_, srcs=[T.msg[:, 0:1]], dsts=[T.info[:, r:r + 1]] * len(later))],
+                           local_sem=T.sem.l1)
+        need("y", ("l1", len(eng)))
+    else:
+        need("y", kcum)
+    k_w = inc(Y.dma_start(T.ws[:], T.w[:]), "lw", 16)
+    k_v = inc(Y.dma_start(T.vsb[:], T.v[:]), "lv", 16)
+    c_xs = iota(T.xs[:, 1024:1040], [[0, 16]], 0)
     if r:
-        v(V.tensor_copy(T.fb[:, r - 1:r], T.row[:, 0:1]))
-    need("v", k, kss)
-    for t in (2, 3, 0, 1):
-        k = v(V.tensor_scalar(T.of[:, NO * t:NO * t + NE], T.ss[:], 2.0, 512.0 + t, Op.mult, Op.add))
-        if t == 3:
-            kof = k
-    need("s", kof)
-    for t in (2, 3):
-        kcs = s_(S.activation(T.ct[:, t:64 * NE:4], T.xs[:, 0:1024].indirect(T.of[:, NO * t:NO * t + NE]), Act.Copy))
+        iota(T.sb[:, 2 * r:2 * r + 2], [[-14, 2]], 0)
+        need("g", iota(T.d0[:], [[0, 24]], 1))
+        c_d0 = iota(T.d0[:, 2 * r:2 * r + 1], [[0, 1]], 4)
+    c_jm = iota(T.jm[:], [[0, 16], [1, 16]], 0)
+
+    need("s", kcum, kthr)
+    for i, c in enumerate(SC):
+        kss = s_(S.activation(T.sg[:, 256 * i + J0:256 * i + 256], T.cum[:, J0:256], Act.Sign, bias=T.thr[:, c:c + 1], scale=-1.0,
+                              accum_out=T.ss[:, c:c + 1]))
+    j0 = [16 * max(c - 1, 0) for c in VC]
+
+    def compare(c, te):
+        return v(V.tensor_scalar(T.cm[:, 256 * c + j0[c]:256 * c + 256], T.cum[:, j0[c]:256], te, 2.0, Op.is_lt, Op.mult))
+
+    def count(c):
+        return v(V.tensor_tensor_scan(T.cs[:, 256 * c + j0[c]:256 * c + 256], T.ones[:, j0[c]:256], T.cm[:, 256 * c + j0[c]:256 * c + 256],
+                                      2.0 * j0[c] - 256 - J0, Op.mult, Op.add))
+
+    need("v", kthr)
+    kte = v(V.tensor_scalar(T.te[:], T.cum[:, 255:256], UP, TOP, Op.add, Op.min))
+    k1 = compare(1, T.thr[:, 1:2])
+    compare(2, T.thr[:, 2:3])
+    k3 = compare(3, T.thr[:, 3:4])
+    need("v", kte)
+    k0 = compare(0, T.te[:])
+    need("v", k1)
+    count(1)
+    need("v", k3)
+    count(2)
+    count(3)
+    need("v", k0)
+    k = count(0)
     need("v", k)
-    for t in (0, 1):
-        kcv = v(V.tensor_copy(T.ct[:, t:64 * NE:4], T.xs[:, 0:1024].indirect(T.of[:, NO * t:NO * t + NE])))
-    need("v", c_hb)
-    kfil = v(V.quantize_mx(T.rc[:, 128:RLAND], T.rp[:, 128:RLAND], T.hb[:, 0:4 * (N - 1) * RW]))
+    k = v(V.tensor_copy(T.ss[:, 0:len(VC)], T.cs[:, 255:256 * len(VC):256]))
+    need("v", k, kss)
+    kof = [v(V.tensor_scalar(T.of[:, NO * t:NO * t + NE], T.ss[:], 2.0, 2.0 * (256 + J0) + t, Op.mult, Op.add)) for t in range(4)]
+    for t in range(4 if r else 2):
+        need("s", kof[t], c_xs)
+        kcv = kcs = s_(S.activation(T.ct[:, t:64 * NE:4], T.xs[:].indirect(T.of[:, NO * t:NO * t + NE]), Act.Copy))
+    for t in range(4 if r else 2, 4):
+        need("v", kof[3], c_xs)
+        kcv = v(V.tensor_copy(T.ct[:, t:64 * NE:4], T.xs[:].indirect(T.of[:, NO * t:NO * t + NE])))
 
     if r:
         need("v", c_d0, ("inf_", r * len(eng)))
@@ -280,23 +317,24 @@ def rank_program(g, core, T, topo):
         need("v", kla)
         k = v(V.tensor_tensor(T.sb[:, 0:r], T.la[:, 0:r], T.fb[:, 0:r], Op.not_equal))
         need("v", k)
-        k = v(V.tensor_tensor_scan(T.so[:, 0:2 * r + 4], T.d0[:, 0:2 * r + 4], T.sb[:, 0:2 * r + 4], 0.0, Op.mult, Op.add))
-        need("v", k)
+        k = v(V.tensor_tensor_scan(T.so[:, 0:2 * r + 4], T.d0[:, 0:2 * r + 4], T.sb[:, 0:2 * r + 4], float(N - r), Op.mult, Op.add))
+        need("v", k, kbase)
         koff = v(V.tensor_scalar(T.off[:], T.base[:], T.so[:, 2 * r:2 * r + 1], T.so[:, 2 * r + 3:2 * r + 4], Op.subtract, Op.add))
     else:
+        need("v", kbase)
         koff = v(V.tensor_copy(T.off[:], T.base[:]))
     need("s", koff, kcs, kcv)
-    kgs = s_(S.activation(T.hs[:, H0 + 2 * NB:H0 + 4 * NB], T.ct[:].indirect(T.off[:, 18:36]), Act.Copy))
+    kgs = s_(S.activation(T.hs[:, 2 * NB:4 * NB], T.ct[:].indirect(T.off[:, 18:36]), Act.Copy))
     need("v", koff, kcs, kcv)
-    kgv = v(V.tensor_copy(T.hs[:, H0:H0 + 2 * NB], T.ct[:].indirect(T.off[:, 0:18])))
+    kgv = v(V.tensor_copy(T.hs[:, 0:2 * NB], T.ct[:].indirect(T.off[:, 0:18])))
     need("v", kgs, kgv)
-    ksq = v(V.quantize_mx(T.sc[:], T.sp[:], T.hs[:, H0:H0 + 4 * NB]))
-    send(T.sc, T.sp, lambda d: W * d + early, T.fc, T.fp, lambda d: slot(d) + early, W - early, "af", ksq)
+    ksq = v(V.quantize_mx(T.fc[:, FM:FM + 128], T.fp[:, FM:FM + 128], T.hs[:, 0:512]))
+    send(ksq, inward(1, 0), inward(1, 1) + direct(1, 0), direct(1, 1))
 
-    k = v(V.memset(T.hs[:, 0:H0], 0.0))
+    need("v", ksq)
+    k = v(V.tensor_copy(T.hs[:, 4 * (NB - RW):4 * (NB - W)], T.xs[:, 0:4 * (RW - W)]))
     need("v", k)
-    i = 4 * (PAD + W * r + W)
-    kown = v(V.quantize_mx(T.fc[:, 0:128], T.fp[:, 0:128], T.hs[:, i - 512:i]))
+    kown = v(V.quantize_mx(T.fc[:, 0:FL], T.fp[:, 0:FL], T.hs[:, 4 * (NB - FL):4 * NB]))
     need("v", k_a)
     kaq = v(V.quantize_mx(T.ac[:], T.apl[:], T.as_[:]))
     need("v", k_w)
@@ -306,51 +344,55 @@ def rank_program(g, core, T, topo):
     need("t", kwq)
     kw = t_(E.matmul_mx(T.ps5[:, 0:256], T.wc[:], T.wp[:], T.xc[:], T.xp[:], True, True))
     need("s", kw)
-    kwy = s_(S.activation(T.wy[:], T.ps5[:, 0:256], Act.Copy))
-    klb0 = s_(S.activation(T.lbt[0:1, 0:256], T.row[0:1, :], Act.Copy))
+    kwy = s_(S.activation(T.wy[:], T.ps5[:, 0:128], Act.Copy))
+    klb0 = s_(S.activation(T.lbt[0:1, 0:256], T.row[0:1, :], Act.Copy, bias=33.0, scale=-1.0))
     need("v", c_jm)
-    k = v(V.tensor_scalar(T.m16[:], T.jm[:], T.fi[:, 0:1], None, Op.is_equal))
-    krm = v(V.memset(T.rm[:], 1.0))
-    need("v", k, krm)
-    krm = v(V.memset(T.rm[:, 0:256:16], 0.0))
-    kc0 = v(V.tensor_tensor(T.cw0[:], T.cum[:], T.m16[:], Op.mult))
-    need("v", krm, kc0)
-    kcw = v(V.tensor_tensor_scan(T.cw1[:], T.rm[:], T.cw0[:], 0.0, Op.mult, Op.add))
-
-    need("t", kaq, kown, ("af", 2 * len(others)), ("ae", 0 if early else 2))
-    ps = [T.ps1, T.ps2, T.ps3, T.ps4]
-    km = [t_(E.matmul_mx(ps[i][:, 0:NB], T.ac[:, 128 * i:128 * i + 128], T.apl[:, 128 * i:128 * i + 128],
-                         T.fc[:, 128 - W:LAND], T.fp[:, 128 - W:LAND], True, True)) for i in range(4)]
-    for i in (0, 2):
-        need("v", km[i])
-        kh = v(V.tensor_scalar(T.hb[:, H0 + i:H0 + 4 * NB:4], ps[i][:, 0:NB], 0.0, 0.05, Op.max, Op.mult))
-    need("s", kfil)
-    for i in (1, 3):
-        need("s", km[i])
-        khs = s_(S.activation(T.hb[:, H0 + i:H0 + 4 * NB:4], ps[i][:, 0:NB], Act.Relu, scale=0.05))
-    need("v", kh, khs)
-    khq = v(V.quantize_mx(T.hc[:], T.hp[:], T.hb[:, H0:H0 + 4 * NB]))
-    send(T.hc, T.hp, lambda d: W * ((d - r) % N) - 1, T.rc, T.rp, lambda d: 128 + RW * ((r - d) % N - 1), W + 1, "ar", khq)
-    k = v(V.tensor_copy(T.hb[:, H0 - 4:H0], T.hb[:, H0 + 4 * NB - 4:H0 + 4 * NB]))
+    k = v(V.tensor_scalar(T.mq[:], T.jm[:], Q, 512.0, Op.is_le, Op.mult))
     need("v", k)
-    i = 4 * (PAD - 1 + RW)
-    krq = v(V.quantize_mx(T.rc[:, 0:128], T.rp[:, 0:128], T.hb[:, i - 512:i]))
+    kcw = v(V.tensor_tensor_scan(T.cw1[:], T.mq[:], T.cum[:], 0.0, Op.add, Op.min))
+
+    ps = [T.ps1, T.ps2, T.ps3, T.ps4]
+    khq = v(V.memset(T.hb[:, 4 * W1:512], 0.0))
+    for a, b, sem in ((0, W1, "af"), (W1, NR, "ag")):
+        need("t", kaq, kown, khq, ("ae", 2 * len(eng)), (sem, 2 * len(eng)))
+        end = FL - RW + b
+        km = [t_(E.matmul_mx(ps[i][:, 0:128], T.ac[:, 128 * i:128 * i + 128], T.apl[:, 128 * i:128 * i + 128],
+                             T.fc[:, end - 128:end], T.fp[:, end - 128:end], True, True)) for i in range(4)]
+        for i in (0, 2):
+            need("v", km[i])
+            kh = v(V.tensor_scalar(T.hb[:, 4 * a + i:4 * b:4], ps[i][:, 128 - b + a:128], 0.0, 0.05, Op.max, Op.mult))
+        for i in (1, 3):
+            need("s", km[i])
+            khs = s_(S.activation(T.hb[:, 4 * a + i:4 * b:4], ps[i][:, 128 - b + a:128], Act.Relu, scale=0.05))
+        need("v", kh, khs)
+        if a:
+            khq = v(V.quantize_mx(T.hc[:, HL - 128:HL], T.hp[:, HL - 128:HL], T.hb[:, 4 * NR - 512:4 * NR]))
+            send(khq, direct(2, 0), direct(2, 1))
+        else:
+            khq = v(V.quantize_mx(T.hc[:, 0:128], T.hp[:, 0:128], T.hb[:, 0:512]))
+            send(khq, inward(2, 0), inward(2, 1))
+    need("t", kvq, khq)
+    k = t_(E.matmul_mx(T.ps0[:, 0:HL], T.vc[:], T.vp[:], T.hc[:, 0:HL], T.hp[:, 0:HL], True, True))
+    need("s", k)
+    s_(S.activation(T.vw[:, 0:2], T.ps0[:, HL - 2:HL], Act.Copy))
+    kvo = s_(S.activation(T.vw[:, 2:RW], T.ps0[:, 0:RW - 2], Act.Copy))
 
     cw = T.cw1[:, 15:256:16]
     if r:
         v(V.tensor_scalar(T.bt[:, 0:1], T.so[:, 2 * r:2 * r + 1], T.so[:, 2 * r + 3:2 * r + 4], 0.25, Op.subtract, Op.mult))
-        kbt = v(V.tensor_scalar(T.bt[:, 1:2], T.sb[:, r - 1:r], -1.0, 1.0 + early, Op.mult, Op.add))
+        kbt = v(V.tensor_scalar(T.bt[:, 1:2], T.sb[:, r - 1:r], -1.0, 3.0, Op.mult, Op.add))
     else:
-        kbt = v(V.memset(T.bt[:, 0:2], 0.0))
+        v(V.memset(T.bt[:, 0:1], 0.0))
+        kbt = v(V.memset(T.bt[:, 1:2], 2.0))
     need("v", kbt, kcw)
-    v(V.tensor_scalar(T.gi[:], cw, T.bt[:, 0:1], None, Op.add))
-    kgr = v(V.tensor_scalar(T.gr[:], cw, T.bt[:, 0:1], float(N - r), Op.add, Op.add))
+    k = v(V.tensor_scalar(T.gr[:], cw, T.bt[:, 0:1], None, Op.add))
     v(V.tensor_scalar(T.z[:], cw, 0.0, T.bt[:, 1:2], Op.is_equal, Op.mult))
-    need("v", kgr)
-    v(V.tensor_scalar(T.h1[:], T.gi[:], 3, 15 if early else 31, Op.logical_shift_right, Op.bitwise_and))
+    need("v", k)
+    v(V.tensor_scalar(T.gi[:], T.gr[:], -1.0, 0.0, Op.add, Op.max))
     k = v(V.tensor_scalar(T.d1[:], T.gr[:], 7, None, Op.bitwise_and))
     need("v", k)
-    k = v(V.tensor_scalar(T.u[:], T.d1[:], float(RW), 1.0 + early, Op.mult, Op.add))
+    v(V.tensor_scalar(T.h1[:], T.gi[:], 3, 15, Op.logical_shift_right, Op.bitwise_and))
+    k = v(V.tensor_scalar(T.u[:], T.d1[:], float(RW), 4.0, Op.mult, Op.add))
     need("v", k)
     k = v(V.tensor_tensor(T.u2[:], T.u[:], T.h1[:], Op.add))
     need("v", k)
@@ -359,11 +401,11 @@ def rank_program(g, core, T, topo):
     kpos = v(V.tensor_copy(T.pos[:], T.u3[:]))
     if r:
         k = v(V.tensor_scalar(T.ni[:, 0:r], T.inf[:, 0:r], 255, None, Op.bitwise_and))
-        v(V.tensor_copy(T.nf[:, r:2 * r], T.sb[:, 0:r]))
+        v(V.tensor_copy(T.nn[:, r:2 * r], T.sb[:, 0:r]))
         need("v", k)
-        k = v(V.tensor_copy(T.nf[:, 0:r], T.ni[:, 0:r]))
+        k = v(V.tensor_copy(T.nn[:, 0:r], T.ni[:, 0:r]))
         need("v", k)
-        k = v(V.tensor_reduce(T.bt[:, 2:3], T.nf[:, 0:2 * r], AxisListType.X, Op.add))
+        k = v(V.tensor_reduce(T.bt[:, 2:3], T.nn[:, 0:2 * r], AxisListType.X, Op.add))
         need("v", k)
         klb = v(V.tensor_scalar(T.lbt[0:1, 256:512], T.cum[0:1, :], T.bt[0:1, 2:3], None, Op.add))
     else:
@@ -371,13 +413,16 @@ def rank_program(g, core, T, topo):
     need("y", klb, klb0)
     kslb = inc(Y.dma_start(T.lb[:], T.lbt[0:1, :]), "slb", 16)
 
-    need("t", kvq, krq, ("ar", 2 * len(others)))
-    kvm = t_(E.matmul_mx(T.ps6[:, 0:NR], T.vc[:], T.vp[:], T.rc[:, 128 - RW:RLAND], T.rp[:, 128 - RW:RLAND], True, True))
+    need("t", kvq, khq, ("ar", 4 * len(eng)))
+    kvm = t_(E.matmul_mx(T.ps6[:, 0:NR - RW], T.vc[:], T.vp[:], T.hc[:, HL:HL + NR - RW], T.hp[:, HL:HL + NR - RW], True, True))
     need("v", kvm)
-    k = v(V.tensor_copy(T.vw[:], T.ps6[:, 0:NR]))
-    need("v", k, kwy, kpos)
-    ky0 = v(V.tensor_tensor(T.yt[:, 0:128], T.vw[:].indirect(T.pos[:, 0:8]), T.wy[:, 0:128], Op.add))
-    ky1 = v(V.tensor_tensor(T.yt[:, 128:256], T.vw[:].indirect(T.pos[:, 8:16]), T.wy[:, 128:256], Op.add))
+    k = v(V.tensor_copy(T.vw[:, RW:NR], T.ps6[:, 0:NR - RW]))
+    need("s", k, kpos, kvo)
+    kg = s_(S.activation(T.vg[:], T.vw[:].indirect(T.pos[:, 8:16]), Act.Copy))
+    need("v", k, kwy, kpos, kvo)
+    ky0 = v(V.tensor_tensor(T.yt[:, 0:128], T.vw[:].indirect(T.pos[:, 0:8]), T.wy[:], Op.add))
+    need("v", kg)
+    ky1 = v(V.tensor_tensor(T.yt[:, 128:256], T.ps5[:, 128:256], T.vg[:], Op.add))
     need("y", ky0)
     ks0 = inc(Y.dma_start(T.y[:, 0:128], T.yt[:, 0:128]), "sy0", 16)
     need("s", ky1)

@@ -2,9 +2,14 @@ from concourse.bass import DstId, RemoteDMATransfer
 from concourse.mybir import dt, AluOpType as Op, AxisListType, ActivationFunctionType as Act
 
 N, TC = 8, 256
-W = 18
-RW = W + 2
+EW = 2
+W = 17
+RW = W + EW
+XO = 144
+YV = 160
 NB, NR = N * W, N * RW
+NG = NB // 4
+LD = NR - RW
 FL, FM = 128, 272
 NE = 9
 NO = NE + 1
@@ -12,54 +17,73 @@ VC, SC = [0, 1, 2, 3], [4, 5, 6, 7, 8]
 J0 = 48
 BIG = 1e29
 RND = 1.5 * 2 ** 23
+R12 = RND * 4096
+HELP = ((2, 2), (1, 2), (1, 2))
+WHOLE = ((0, 0), (1, 0), (1, 1))
 NEAR = 3
-W1 = RW * (NEAR + 1)
-HL = 256
+W1, W2 = RW * (NEAR + 1) + 1, RW * (N - 1 - NEAR) + 2
+HA, HL = 512, 256
 RELAY = [list(range(1, N)), list(range(1, N - NEAR)), list(range(1, NEAR + 1))]
 DIRECT = [[b for b in range(1, N) if b not in bs] for bs in RELAY]
 
 SCRATCH = {}
 for _n, _w, _t in (
         ("xs", 1040, "bfloat16"), ("pst", 576, "bfloat16"), ("as_", 2048, "bfloat16"), ("ws", 512, "bfloat16"), ("vsb", 512, "bfloat16"),
-        ("tr", 128, "float32"), ("pm", 132, "float32"), ("mk", 128, "float32"), ("nf", 128, "bfloat16"), ("dd", 144, "bfloat16"),
-        ("ta", 288, "bfloat16"), ("mh", 128, "bfloat16"), ("bc", 256, "bfloat16"), ("row", 256, "bfloat16"),
+        ("tr", 128, "float32"), ("pm", 132, "float32"), ("mk", 64, "float32"), ("nf", 128, "bfloat16"), ("dd", 144, "bfloat16"),
+        ("ta", 304, "bfloat16"), ("mh", 128, "bfloat16"), ("bc", 256, "bfloat16"), ("row", 256, "bfloat16"),
         ("df", 256, "bfloat16"), ("sf", 256, "bfloat16"), ("cum", 256, "bfloat16"), ("ones", 256, "bfloat16"),
-        ("tp", 2, "float32"), ("msg", 2, "uint16"),
+        ("tp", 4, "float32"), ("msg", 2, "uint16"),
         ("tb", 160, "bfloat16"), ("fi", 160, "bfloat16"), ("th1", NE, "float32"), ("th0", NE, "float32"), ("thr", NE, "float32"), ("te", 1, "float32"),
         ("ss", NE, "float32"), ("sg", 256 * len(SC), "bfloat16"), ("cm", 256 * len(VC), "bfloat16"), ("cs", 256 * len(VC), "bfloat16"),
-        ("of", 4 * NO, "uint16"), ("ct", 64 * NE, "bfloat16"), ("q0", 36, "float32"), ("q", 36, "float32"), ("qm", 36, "float32"),
-        ("qd", 36, "float32"), ("qe", 36, "float32"), ("b1", 36, "float32"), ("b2", 36, "float32"), ("b3", 36, "float32"), ("b4", 36, "float32"),
-        ("b5", 36, "float32"), ("base", 36, "float32"), ("off", 36, "uint16"), ("info", 8, "uint16"), ("inf", 8, "int32"),
+        ("of", 4 * NO, "uint16"), ("ct", 64 * NE, "bfloat16"), ("q0", NG, "float32"), ("q", NG, "float32"), ("qm", NG, "float32"),
+        ("qd", NG, "float32"), ("qe", NG, "float32"), ("b1", NG, "float32"), ("b2", NG, "float32"), ("b3", NG, "float32"), ("b4", NG, "float32"),
+        ("b5", NG, "float32"), ("base", NG, "float32"), ("off", NG, "uint16"), ("info", 8, "uint16"), ("inf", 8, "int32"),
         ("la", 8, "int32"), ("fb", 8, "int32"), ("sb", 24, "float32"), ("d0", 24, "float32"), ("so", 24, "float32"),
-        ("hs", 4 * NB, "bfloat16"), ("hb", 4 * NR, "bfloat16"),
+        ("hs", 4 * NB, "bfloat16"), ("hb", 4 * HL, "bfloat16"),
         ("jm", 256, "bfloat16"), ("mq", 256, "bfloat16"), ("cw1", 256, "bfloat16"),
         ("bt", 4, "float32"), ("gi", 16, "int32"), ("gr", 16, "int32"), ("h1", 16, "int32"), ("d1", 16, "int32"), ("z", 16, "float32"),
         ("u", 16, "float32"), ("u2", 16, "float32"), ("pos", 16, "uint16"), ("u3", 16, "float32"), ("ni", 8, "int32"), ("nn", 16, "float32"),
-        ("lbt", 512, "float32"), ("wy", 128, "float32"), ("vw", NR, "float32"), ("vg", 128, "float32"), ("yt", 256, "float32")):
+        ("lbt", 512, "float32"), ("wy", YV, "float32"), ("vw", NR, "float32"), ("vg", 256 - YV, "float32"), ("yt", 256, "float32")):
     SCRATCH[_n] = ("sbuf", [128, _w], _t)
-for _n, _m, _w in (("pc", "pp", 144), ("xc", "xp", 256), ("ac", "apl", 512), ("wc", "wp", 128), ("vc", "vp", 128),
-                   ("fc", "fp", FM + 128), ("hc", "hp", HL + NR - RW)):
+for _n, _m, _w in (("xc", "xp", XO + 256), ("wc", "wp", 128), ("vc", "vp", 128),
+                   ("fc", "fp", FM + 128), ("hc", "hp", HA + HL + LD + 2)):
     SCRATCH[_n] = ("sbuf", [128, _w], "float8_e4m3fn_x4")
     SCRATCH[_m] = ("sbuf", [128, _w], "uint8")
-for _i in range(7):
+for _i in range(8):
     SCRATCH["ps%d" % _i] = ("psum", [128, 512], "float32")
 SEMAPHORES = ["v", "s", "t", "gc", "lp", "lxa", "lxb", "la_", "lw", "lv", "inf_", "af", "ar", "loc", "sy0", "sy1", "slb",
-              "l1", "r0", "r1", "r2", "ag", "ae"]
+              "lc", "in0", "r0", "r1", "r2", "ag", "ae"]
 
 
 def helpers(core, T, topo):
-    return [c for c in topo.cores_of(core) if topo.die(c) != topo.die(core)
-            and all(topo.may_write(c, d) for d in T.cores if d != core)][:2]
+    near = sorted((c for c in topo.cores_of(core) if c != core), key=lambda c: topo.die(c) != topo.die(core))
+    free = [c for c in near if all(topo.may_write(c, d) for d in T.cores if d != core)]
+    bound = [c for c in near if c not in free]
+    return [[free[what], bound[what]] for what in (0, 1)]
+
+
+def served(T, topo, r, j, what, i):
+    last = helpers(T.cores[r], T, topo)[what][HELP[j][what] - 1]
+    return [b for b in RELAY[j] if topo.may_write(last, T.cores[(r + b) % N]) == (i == HELP[j][what] - 1)]
+
+
+def relayed(T, topo, r, j):
+    total = 0
+    for b in RELAY[j]:
+        s = (r - b) % N
+        for what in (0, 1):
+            for i in range(HELP[j][what]):
+                bs = served(T, topo, s, j, what, i)
+                if b in bs:
+                    total += shares(topo.engines(T.cores[s], T.cores[r]), len(bs), what)[1][bs.index(b)]
+    return total
 
 
 def steps(T):
     xs, fs, hs = (T.xc, T.xp), (T.fc, T.fp), (T.hc, T.hp)
-    return ((xs, lambda b: 0, fs, lambda b: FL + RW * (N - b - 1), RW - W, "ae", "ae"),
+    return ((xs, lambda b: XO - 1, fs, lambda b: FL + RW * (N - b - 1), RW - W, "ae", "ae"),
             (fs, lambda b: FM + W * (b - 1), fs, lambda b: FL + RW * (N - b) - W, W, "af", "ag"),
-            (hs, lambda b: RW * b - 2 + (HL - NR) * (b > NEAR), hs, lambda b: HL + RW * (N - b - 1), RW, "ar", "ar"))
-
-
-WHOLE = [(False, False), (True, False), (True, True)]
+            (hs, lambda b: HA + RW * b - 1 + (HL - NR - 1) * (b > NEAR), hs, lambda b: HA + HL + RW * (N - b - 1), RW, "ar", "ar"))
 
 
 def view(bufs, what, a, w):
@@ -81,27 +105,29 @@ def shares(eng, n, turn):
 def outward(T, topo, core, r, j, what, bs, which):
     src, at, to, land, w = steps(T)[j][:5]
     tr = []
-    for b, m in zip(bs, shares(topo.engines(core, T.cores[(r + 1) % N]), len(bs), what)[0]):
+    for b, m in zip(bs, shares(topo.engines(core, T.cores[(r + bs[0]) % N]), len(bs), what)[0]):
         rid, pid = topo.addr(T.cores[(r + b) % N], core)
         tr.append(RemoteDMATransfer(dst_ids=[DstId(rid=rid, pnc=pid)], dma_engine_mask=m, remote_sem=T.sem[steps(T)[j][5 + which]],
                                     srcs=[view(src, what, at(b), w)], dsts=[view(to, what, land(b), w)]))
     return tr
 
 
-def helper_program(g, core, T, topo, r, what):
-    out = len(topo.engines(core, T.cores[(r + 1) % N]))
-    for j in range(3):
+def helper_program(g, core, T, topo, r, what, i):
+    out = len(topo.engines(T.cores[r], T.cores[(r + 1) % N]))
+    mine = [j for j in range(3) if i < HELP[j][what]]
+    for j in mine:
         g.wait_ge(T.sem["r%d" % j], len(topo.engines(T.cores[r], core)) - (0 if WHOLE[j][what] else out))
-        g.remote_dma_fused(outward(T, topo, core, r, j, what, RELAY[j], 1), local_sem=T.sem.loc)
-    g.wait_ge(T.sem.loc, 3 * out)
+        g.remote_dma_fused(outward(T, topo, core, r, j, what, served(T, topo, r, j, what, i), 1), local_sem=T.sem.loc)
+    g.wait_ge(T.sem.loc, len(mine) * out)
 
 
 def rank_program(g, core, T, topo):
     r = T.rank_of(core)
     if r is None:
         for i, c in enumerate(T.cores):
-            if core in topo.cores_of(c) and core in helpers(c, T, topo):
-                helper_program(g, core, T, topo, i, helpers(c, T, topo).index(core))
+            for what, cores in enumerate(helpers(c, T, topo)):
+                if core in cores:
+                    helper_program(g, core, T, topo, i, what, cores.index(core))
         return
     V, S, E, Y = g.vector, g.scalar, g.tensor, g.sync
     queues = {"v": V, "s": S, "t": E, "y": Y, "g": g}
@@ -135,11 +161,14 @@ def rank_program(g, core, T, topo):
 
     def inward(j, what):
         src, at, w = steps(T)[j][0], steps(T)[j][1], steps(T)[j][4]
-        run = view(src, what, at(1), w * (len(RELAY[j]) if j else 1 + 3 * what))
-        use = [e for e in topo.engines(core, hlp[what]) if WHOLE[j][what] or (e in eng) == (j + what == 0)]
+        a, w = at(1), w * (len(RELAY[j]) if j else 1)
+        if what and j < 2:
+            w = 4 * steps(T)[j][4]
+        run = view(src, what, a, w)
+        use = [e for e in topo.engines(core, hlp[what][0]) if WHOLE[j][what] or (e in eng) == (j + what == 0)]
         cnt["loc"] = cnt.get("loc", 0) + len(use)
-        return [RemoteDMATransfer(dst_ids=[dst(hlp[what])], dma_engine_mask=sum(1 << e for e in use), remote_sem=T.sem["r%d" % j],
-                                  srcs=[run], dsts=[run])]
+        return [RemoteDMATransfer(dst_ids=[dst(h) for h in hlp[what][:HELP[j][what]]], dma_engine_mask=sum(1 << e for e in use),
+                                  remote_sem=T.sem["r%d" % j], srcs=[run], dsts=[run] * HELP[j][what])]
 
     def direct(j, what):
         cnt["loc"] = cnt.get("loc", 0) + len(eng)
@@ -153,8 +182,6 @@ def rank_program(g, core, T, topo):
     k_p = inc(S.dma_start(T.pst[:, 64:192], T.p[:, 0:128]), "lp", 16)
     k_xa = inc(Y.dma_start(T.xs[:, 0:512], T.x[:, 0:512]), "lxa", 16)
     k_xb = inc(S.dma_start(T.xs[:, 512:1024], T.x[:, 512:1024]), "lxb", 16)
-    need("y", k_xa, k_xb)
-    k_a = inc(Y.dma_start(T.as_[:], T.a[:]), "la_", 16)
 
     def iota(out, pattern, base):
         return gc(g.iota(out, pattern, base, 0, allow_small_or_imprecise_dtypes=True))
@@ -162,9 +189,10 @@ def rank_program(g, core, T, topo):
     for i, (pattern, base) in enumerate((([[0, 2], [1, 16]], 0), ([[0, 2], [1, 4], [0, 4]], 0), ([[0, 8], [1, 4]], 28),
                                          ([[0, 2], [128, 2], [0, 8]], 0), ([[0, 2], [-120, 2], [1, 8]], 241))):
         c_tb = iota(T.tb[:, 32 * i:32 * i + 32], pattern, base)
-    c_q0 = iota(T.q0[:], [[4, 36]], 0)
+    c_q0 = iota(T.q0[:], [[4, NG]], 0)
     c_th = iota(T.th0[:], [[16, NE]], -15)
-    c_ta = iota(T.ta[:, 256:288], [[0, 32]], 0)
+    iota(T.ta[:, 128:144], [[0, 16]], 0)
+    c_ta = iota(T.ta[:, 272:304], [[0, 32]], 0)
     Q, Q4, T28, UP, TOP = (T.fi[:, 32 * i:32 * i + 1] for i in range(5))
 
     kz = v(V.memset(T.pst[:, 0:64], 0.0))
@@ -175,7 +203,11 @@ def rank_program(g, core, T, topo):
     need("v", m1)
     v(V.memset(T.dd[:, 15:144:32], 18.0))
     v(V.memset(T.mh[:, 0:128:32], -128.0))
-    m4 = v(V.memset(T.mk[:, 15:128:16], -BIG))
+    m4 = v(V.memset(T.mk[:, 15:64:16], -BIG))
+    v(V.memset(T.df[:, 0:1], 0.0))
+    if r:
+        v(V.memset(T.sb[:, 2 * r + 2:2 * r + 3], 402653184.0))
+        v(V.memset(T.sb[:, 2 * r + 3:2 * r + 4], -402653184.0))
     need("s", k_p)
     cp = [s_(S.activation(T.pst[:, 64 + 128 * k:192 + 128 * k], T.pst[:, 64:192], Act.Copy)) for k in (1,)]
     need("v", c_tb)
@@ -196,57 +228,62 @@ def rank_program(g, core, T, topo):
     v(V.tensor_copy(T.pst[:, 320:448], T.pst[:, 64:192]))
     k = v(V.tensor_copy(T.pst[:, 448:576], T.pst[:, 64:192]))
     need("v", k, cp[-1], kz)
-    v(V.quantize_mx(T.pc[:], T.pp[:], T.pst[:]))
+    v(V.quantize_mx(T.xc[:, 0:XO], T.xp[:, 0:XO], T.pst[:]))
     need("v", k_xa)
-    kx0 = v(V.quantize_mx(T.xc[:, 0:128], T.xp[:, 0:128], T.xs[:, 0:512]))
+    kx0 = v(V.quantize_mx(T.xc[:, XO:XO + 128], T.xp[:, XO:XO + 128], T.xs[:, 0:512]))
     need("v", k_xb)
-    kx = v(V.quantize_mx(T.xc[:, 128:256], T.xp[:, 128:256], T.xs[:, 512:1024]))
+    kx = v(V.quantize_mx(T.xc[:, XO + 128:], T.xp[:, XO + 128:], T.xs[:, 512:1024]))
     need("t", kx0)
-    E.matmul_mx(T.ps0[:, 0:128], T.pc[:, 16:144], T.pp[:, 16:144], T.xc[:, 0:128], T.xp[:, 0:128], True, False)
+    E.matmul_mx(T.ps0[:, 0:128], T.xc[:, 16:XO], T.xp[:, 16:XO], T.xc[:, XO:XO + 128], T.xp[:, XO:XO + 128], True, False)
     need("t", kx)
-    ks = t_(E.matmul_mx(T.ps0[:, 0:128], T.pc[:, 0:128], T.pp[:, 0:128], T.xc[:, 128:256], T.xp[:, 128:256], False, True))
+    ks = t_(E.matmul_mx(T.ps0[:, 0:128], T.xc[:, 0:128], T.xp[:, 0:128], T.xc[:, XO + 128:], T.xp[:, XO + 128:], False, True))
+    need("y", kx0)
+    for bufs, a in (((T.fc, T.fp), FL + LD), ((T.hc, T.hp), HA + HL + LD)):
+        for what in (0, 1):
+            k_c0 = inc(Y.dma_start(view(bufs, what, a, 2), view((T.xc, T.xp), what, XO, 2)), "lc", 16)
+    need("y", k_xb)
+    k_a = inc(Y.dma_start(T.as_[:], T.a[:]), "la_", 16)
+    k_w = inc(Y.dma_start(T.ws[:], T.w[:]), "lw", 16)
+    k_v = inc(Y.dma_start(T.vsb[:], T.v[:]), "lv", 16)
     send(kx0, inward(0, 0) + inward(0, 1))
     v(V.memset(T.ones[:], 1.0))
-    v(V.memset(T.df[:, 0:1], 0.0))
 
-    need("v", ks, m4)
-    k = v(V.transpose(T.tr[:], T.ps0[:, 0:128]))
+    def halves(after, call):
+        done = []
+        for h in (0, 1):
+            need("v", after[h])
+            done.append(v(call(h)))
+        return done
+
+    need("v", m4, c_ta)
+    k = halves((ks, ks), lambda h: V.transpose(T.tr[:, 64 * h:64 * h + 64], T.ps0[:, 64 * h:64 * h + 64]))
+    k = halves(k, lambda h: V.tensor_tensor_scan(T.pm[:, 64 * h + 1:64 * h + 65], T.tr[:, 64 * h:64 * h + 64], T.mk[:], -BIG,
+                                                 Op.max, Op.add))
+    k = halves(k, lambda h: V.tensor_tensor(T.nf[:, 64 * h:64 * h + 64], T.pm[:, 64 * h:64 * h + 64], T.tr[:, 64 * h:64 * h + 64],
+                                            Op.is_ge))
     need("v", ks_)
     kb = v(V.tensor_tensor(T.b3[:], T.b1[:], T.b2[:], Op.add))
-    need("v", k)
-    k = v(V.tensor_tensor_scan(T.pm[:, 1:129], T.tr[:], T.mk[:], -BIG, Op.max, Op.add))
-    need("v", kb)
-    kb = v(V.tensor_scalar(T.b4[:], T.b3[:], 137.0, None, Op.is_lt))
-    need("v", k)
-    k = v(V.tensor_tensor(T.nf[:], T.pm[:, 0:128], T.tr[:], Op.is_ge))
-    need("v", kb)
-    kb5 = v(V.tensor_tensor(T.b5[:], T.b3[:], T.b4[:], Op.mult))
-    need("v", k, c_ta)
-    v(V.tensor_tensor_scan(T.ta[:, 0:128], T.nf[:], T.dd[:, 0:128], 0.0, Op.mult, Op.add))
-    k = v(V.tensor_tensor_scan(T.ta[:, 128:256], T.nf[:], T.dd[:, 16:144], 0.0, Op.mult, Op.add))
-    if r:
-        v(V.memset(T.sb[:, 2 * r + 2:2 * r + 3], 402653184.0))
-    need("v", k)
-    v(V.tensor_tensor_scan(T.bc[:, 0:128], T.mh[:], T.ta[:, 15:143], 0.0, Op.add, Op.max))
-    k = v(V.tensor_tensor_scan(T.bc[:, 128:256], T.mh[:], T.ta[:, 159:287], 0.0, Op.add, Op.max))
-    if r:
-        v(V.memset(T.sb[:, 2 * r + 3:2 * r + 4], -402653184.0))
-    need("v", k)
-    krow = v(V.transpose(T.row[:], T.bc[:]))
-    need("v", krow)
-    k = v(V.tensor_tensor_scan(T.df[:, 1:256], T.row[:, 1:256], T.row[:, 0:255], 0.0, Op.max, Op.subtract))
-    if r:
+    k = halves((k[1], k[1]), lambda h: V.tensor_tensor_scan(T.ta[:, 144 * h:144 * h + 128], T.nf[:], T.dd[:, 16 * h:16 * h + 128], 0.0,
+                                                            Op.mult, Op.add))
+    k = halves(k, lambda h: V.tensor_tensor_scan(T.bc[:, 128 * h:128 * h + 128], T.mh[:], T.ta[:, 160 * h + 15:160 * h + 143], 0.0,
+                                                 Op.add, Op.max))
+    k = halves(k, lambda h: V.transpose(T.row[:, 128 * h:128 * h + 128], T.bc[:, 128 * h:128 * h + 128]))
+    krow = k[1]
+    k = halves(k, lambda h: V.tensor_tensor_scan(T.df[:, 127 * h + 1:128 * h + 128], T.row[:, 127 * h + 1:128 * h + 128],
+                                                 T.row[:, 127 * h:128 * h + 127], 0.0, Op.max, Op.subtract))
+    k = halves(k, lambda h: V.tensor_scalar(T.sf[:, 128 * h:128 * h + 128], T.df[:, 128 * h:128 * h + 128], 0.0, None, Op.not_equal))
+    v(V.tensor_scalar(T.b4[:], T.b3[:], 137.0, None, Op.is_lt))
+    need("v", k[1])
+    kcum = v(V.tensor_tensor_scan(T.cum[:], T.ones[:], T.sf[:], 0.0, Op.mult, Op.add))
+    if r == 1:
+        v(V.tensor_scalar(T.tp[:, 2:3], T.row[:, 0:1], 4096.0, R12 - 18.0 * 4096, Op.mult, Op.add))
+    elif r:
         v(V.tensor_scalar(T.fb[:, r - 1:r], T.row[:, 0:1], -18.0, None, Op.add))
-    need("s", kb5)
-    kbase = s_(S.activation(T.base[:], T.b5[:], Act.Identity, bias=T28, scale=4.0))
     need("s", krow)
-    k1 = s_(S.activation(T.tp[:, 0:1], T.row[:, 0:1], Act.Copy, bias=-18.0 * 4352, scale=256.0))
+    first = 256.0 if r else 0.0
+    k1 = s_(S.activation(T.tp[:, 0:1], T.row[:, 0:1], Act.Copy, bias=-18.0 * (4096 + first), scale=first))
     need("s", k1)
     ktp = s_(S.activation(T.tp[:, 1:2], T.row[:, 255:256], Act.Identity, bias=T.tp[:, 0:1], scale=4096.0))
-    need("v", k)
-    k = v(V.tensor_scalar(T.sf[:], T.df[:], 0.0, None, Op.not_equal))
-    need("v", k)
-    kcum = v(V.tensor_tensor_scan(T.cum[:], T.ones[:], T.sf[:], 0.0, Op.mult, Op.add))
     need("v", kcum)
     if r < N - 1:
         need("v", ktp)
@@ -254,13 +291,9 @@ def rank_program(g, core, T, topo):
         need("g", kmsg)
         later = list(range(N - 1, r, -1))
         g.remote_dma_fused([RemoteDMATransfer(dst_ids=[dst(T.cores[d]) for d in later], dma_engine_mask=sum(1 << e for e in eng),
-                                              remote_sem=T.sem.inf_, srcs=[T.msg[:, 0:1]], dsts=[T.info[:, r:r + 1]] * len(later))],
-                           local_sem=T.sem.l1)
-        need("y", ("l1", len(eng)))
-    else:
-        need("y", kcum)
-    k_w = inc(Y.dma_start(T.ws[:], T.w[:]), "lw", 16)
-    k_v = inc(Y.dma_start(T.vsb[:], T.v[:]), "lv", 16)
+                                              remote_sem=T.sem["inf_" if r else "in0"], srcs=[T.msg[:, 0:1]], dsts=[T.info[:, r:r + 1]] * len(later))],
+                           local_sem=T.sem.loc)
+        cnt["loc"] += len(eng)
     c_xs = iota(T.xs[:, 1024:1040], [[0, 16]], 0)
     if r:
         iota(T.sb[:, 2 * r:2 * r + 2], [[-14, 2]], 0)
@@ -295,10 +328,17 @@ def rank_program(g, core, T, topo):
     count(3)
     need("v", k0)
     k = count(0)
+    v(V.tensor_tensor(T.b5[:], T.b3[:], T.b4[:], Op.mult))
     need("v", k)
-    k = v(V.tensor_copy(T.ss[:, 0:len(VC)], T.cs[:, 255:256 * len(VC):256]))
-    need("v", k, kss)
-    kof = [v(V.tensor_scalar(T.of[:, NO * t:NO * t + NE], T.ss[:], 2.0, 2.0 * (256 + J0) + t, Op.mult, Op.add)) for t in range(4)]
+    kof = []
+    for t in range(4):
+        for a, b, ss in ((0, len(VC), T.cs[:, 255:256 * len(VC):256]), (len(VC), NE, T.ss[:, len(VC):NE])):
+            if a:
+                need("v", kss)
+            k = v(V.tensor_scalar(T.of[:, NO * t + a:NO * t + b], ss, 2.0, 2.0 * (256 + J0) + t, Op.mult, Op.add))
+        kof.append(k)
+    need("v", kof[0])
+    kbase = v(V.tensor_scalar(T.base[:], T.b5[:], 4.0, T28, Op.mult, Op.add))
     for t in range(4 if r else 2):
         need("s", kof[t], c_xs)
         kcv = kcs = s_(S.activation(T.ct[:, t:64 * NE:4], T.xs[:].indirect(T.of[:, NO * t:NO * t + NE]), Act.Copy))
@@ -307,15 +347,22 @@ def rank_program(g, core, T, topo):
         kcv = v(V.tensor_copy(T.ct[:, t:64 * NE:4], T.xs[:].indirect(T.of[:, NO * t:NO * t + NE])))
 
     if r:
-        need("v", c_d0, ("inf_", r * len(eng)))
-        k = v(V.tensor_copy(T.inf[:, 0:r], T.info[:, 0:r]))
-        v(V.tensor_copy(T.sb[:, r:2 * r], T.info[:, 0:r]))
-        need("v", k)
-        kla = v(V.tensor_scalar(T.la[:, 0:r], T.inf[:, 0:r], 12, None, Op.logical_shift_right))
-        if r > 1:
-            kla = v(V.tensor_scalar(T.fb[:, 0:r - 1], T.inf[:, 1:r], 8, 15, Op.logical_shift_right, Op.bitwise_and))
-        need("v", kla)
-        k = v(V.tensor_tensor(T.sb[:, 0:r], T.la[:, 0:r], T.fb[:, 0:r], Op.not_equal))
+        need("v", c_d0)
+        if r == 1:
+            need("v", ("in0", len(eng)))
+            v(V.tensor_scalar(T.sb[:, 0:1], T.info[:, 0:1], R12, T.tp[:, 2:3], Op.add, Op.not_equal))
+            k = v(V.tensor_copy(T.sb[:, 1:2], T.info[:, 0:1]))
+        else:
+            need("v", ("inf_", (r - 1) * len(eng)))
+            k = v(V.tensor_copy(T.inf[:, 1:r], T.info[:, 1:r]))
+            need("v", k)
+            v(V.tensor_scalar(T.la[:, 1:r], T.inf[:, 1:r], 12, None, Op.logical_shift_right))
+            v(V.tensor_scalar(T.fb[:, 0:r - 1], T.inf[:, 1:r], 8, 15, Op.logical_shift_right, Op.bitwise_and))
+            need("v", ("in0", len(eng)))
+            k = v(V.tensor_scalar(T.la[:, 0:1], T.info[:, 0:1], 1.0 / 4096, None, Op.mult))
+            v(V.tensor_copy(T.sb[:, r:2 * r], T.info[:, 0:r]))
+            need("v", k)
+            k = v(V.tensor_tensor(T.sb[:, 0:r], T.la[:, 0:r], T.fb[:, 0:r], Op.not_equal))
         need("v", k)
         k = v(V.tensor_tensor_scan(T.so[:, 0:2 * r + 4], T.d0[:, 0:2 * r + 4], T.sb[:, 0:2 * r + 4], float(N - r), Op.mult, Op.add))
         need("v", k, kbase)
@@ -324,66 +371,67 @@ def rank_program(g, core, T, topo):
         need("v", kbase)
         koff = v(V.tensor_copy(T.off[:], T.base[:]))
     need("s", koff, kcs, kcv)
-    kgs = s_(S.activation(T.hs[:, 2 * NB:4 * NB], T.ct[:].indirect(T.off[:, 18:36]), Act.Copy))
+    kgs = s_(S.activation(T.hs[:, 256:512], T.ct[:].indirect(T.off[:, 16:32]), Act.Copy))
+    kgo = s_(S.activation(T.hs[:, 512:4 * NB], T.ct[:].indirect(T.off[:, 32:NG]), Act.Copy))
     need("v", koff, kcs, kcv)
-    kgv = v(V.tensor_copy(T.hs[:, 0:2 * NB], T.ct[:].indirect(T.off[:, 0:18])))
+    kgv = v(V.tensor_copy(T.hs[:, 0:256], T.ct[:].indirect(T.off[:, 0:16])))
     need("v", kgs, kgv)
     ksq = v(V.quantize_mx(T.fc[:, FM:FM + 128], T.fp[:, FM:FM + 128], T.hs[:, 0:512]))
     send(ksq, inward(1, 0), inward(1, 1) + direct(1, 0), direct(1, 1))
+    kfill = iota(T.hb[:, 4 * W1:4 * (HL - W2)], [[0, 4 * (HL - W1 - W2)]], 0)
 
-    need("v", ksq)
-    k = v(V.tensor_copy(T.hs[:, 4 * (NB - RW):4 * (NB - W)], T.xs[:, 0:4 * (RW - W)]))
-    need("v", k)
-    kown = v(V.quantize_mx(T.fc[:, 0:FL], T.fp[:, 0:FL], T.hs[:, 4 * (NB - FL):4 * NB]))
     need("v", k_a)
-    kaq = v(V.quantize_mx(T.ac[:], T.apl[:], T.as_[:]))
-    need("v", k_w)
-    kwq = v(V.quantize_mx(T.wc[:], T.wp[:], T.ws[:]))
-    need("v", k_v)
-    kvq = v(V.quantize_mx(T.vc[:], T.vp[:], T.vsb[:]))
-    need("t", kwq)
-    kw = t_(E.matmul_mx(T.ps5[:, 0:256], T.wc[:], T.wp[:], T.xc[:], T.xp[:], True, True))
-    need("s", kw)
-    kwy = s_(S.activation(T.wy[:], T.ps5[:, 0:128], Act.Copy))
+    kaq = v(V.quantize_mx(T.hc[:, 0:HA], T.hp[:, 0:HA], T.as_[:]))
+    need("v", kgo)
+    kown = v(V.quantize_mx(T.fc[:, 0:FL], T.fp[:, 0:FL], T.hs[:, 4 * (NB - FL):4 * NB]))
     klb0 = s_(S.activation(T.lbt[0:1, 0:256], T.row[0:1, :], Act.Copy, bias=33.0, scale=-1.0))
     need("v", c_jm)
     k = v(V.tensor_scalar(T.mq[:], T.jm[:], Q, 512.0, Op.is_le, Op.mult))
     need("v", k)
     kcw = v(V.tensor_tensor_scan(T.cw1[:], T.mq[:], T.cum[:], 0.0, Op.add, Op.min))
 
-    ps = [T.ps1, T.ps2, T.ps3, T.ps4]
-    khq = v(V.memset(T.hb[:, 4 * W1:512], 0.0))
-    for a, b, sem in ((0, W1, "af"), (W1, NR, "ag")):
-        need("t", kaq, kown, khq, ("ae", 2 * len(eng)), (sem, 2 * len(eng)))
-        end = FL - RW + b
-        km = [t_(E.matmul_mx(ps[i][:, 0:128], T.ac[:, 128 * i:128 * i + 128], T.apl[:, 128 * i:128 * i + 128],
+    for wave, (w, at, end, sem) in enumerate(((W1, 0, FL - RW + W1, "af"), (W2, HL - W2, FL + LD + 1, "ag"))):
+        need("t", kaq, kown, k_c0, ("ae", relayed(T, topo, r, 0)), (sem, relayed(T, topo, r, 1) if wave else 2 * len(eng)))
+        ps = [T["ps%d" % (4 * wave + i)] for i in range(4)]
+        km = [t_(E.matmul_mx(ps[i][:, 0:128], T.hc[:, 128 * i:128 * i + 128], T.hp[:, 128 * i:128 * i + 128],
                              T.fc[:, end - 128:end], T.fp[:, end - 128:end], True, True)) for i in range(4)]
-        for i in (0, 2):
-            need("v", km[i])
-            kh = v(V.tensor_scalar(T.hb[:, 4 * a + i:4 * b:4], ps[i][:, 128 - b + a:128], 0.0, 0.05, Op.max, Op.mult))
-        for i in (1, 3):
+        need("v", km[2])
+        kh = v(V.tensor_scalar(T.hb[:, 4 * at + 2:4 * (at + w):4], ps[2][:, 128 - w:128], 0.0, 0.05, Op.max, Op.mult))
+        for i in (0, 1, 3):
             need("s", km[i])
-            khs = s_(S.activation(T.hb[:, 4 * a + i:4 * b:4], ps[i][:, 128 - b + a:128], Act.Relu, scale=0.05))
-        need("v", kh, khs)
-        if a:
-            khq = v(V.quantize_mx(T.hc[:, HL - 128:HL], T.hp[:, HL - 128:HL], T.hb[:, 4 * NR - 512:4 * NR]))
+            khs = s_(S.activation(T.hb[:, 4 * at + i:4 * (at + w):4], ps[i][:, 128 - w:128], Act.Relu, scale=0.05))
+        need("v", kh, khs, kfill)
+        a = HA + 128 * wave
+        khq = v(V.quantize_mx(T.hc[:, a:a + 128], T.hp[:, a:a + 128], T.hb[:, 512 * wave:512 * wave + 512]))
+        if wave:
             send(khq, direct(2, 0), direct(2, 1))
         else:
-            khq = v(V.quantize_mx(T.hc[:, 0:128], T.hp[:, 0:128], T.hb[:, 0:512]))
             send(khq, inward(2, 0), inward(2, 1))
-    need("t", kvq, khq)
-    k = t_(E.matmul_mx(T.ps0[:, 0:HL], T.vc[:], T.vp[:], T.hc[:, 0:HL], T.hp[:, 0:HL], True, True))
-    need("s", k)
-    s_(S.activation(T.vw[:, 0:2], T.ps0[:, HL - 2:HL], Act.Copy))
-    kvo = s_(S.activation(T.vw[:, 2:RW], T.ps0[:, 0:RW - 2], Act.Copy))
-
-    cw = T.cw1[:, 15:256:16]
+    need("v", k_w, k_v)
+    kwq = v(V.quantize_mx(T.wc[:], T.wp[:], T.ws[:]))
+    kvq = v(V.quantize_mx(T.vc[:], T.vp[:], T.vsb[:]))
     if r:
+        k = v(V.tensor_copy(T.inf[:, 0:1], T.info[:, 0:1]))
         v(V.tensor_scalar(T.bt[:, 0:1], T.so[:, 2 * r:2 * r + 1], T.so[:, 2 * r + 3:2 * r + 4], 0.25, Op.subtract, Op.mult))
-        kbt = v(V.tensor_scalar(T.bt[:, 1:2], T.sb[:, r - 1:r], -1.0, 3.0, Op.mult, Op.add))
+        kbt = v(V.tensor_scalar(T.bt[:, 1:2], T.sb[:, r - 1:r], -2.0, 3.0, Op.mult, Op.add))
+        need("v", k)
+        v(V.tensor_scalar(T.ni[:, 0:r], T.inf[:, 0:r], 255, None, Op.bitwise_and))
+        v(V.tensor_copy(T.nn[:, r:2 * r], T.sb[:, 0:r]))
     else:
         v(V.memset(T.bt[:, 0:1], 0.0))
-        kbt = v(V.memset(T.bt[:, 1:2], 2.0))
+        kbt = v(V.memset(T.bt[:, 1:2], 1.0))
+    need("t", kwq)
+    kw = t_(E.matmul_mx(T.ps1[:, 0:256], T.wc[:], T.wp[:], T.xc[:, XO:], T.xp[:, XO:], True, True))
+    need("t", kvq, khq)
+    k = t_(E.matmul_mx(T.ps0[:, 0:HL], T.vc[:], T.vp[:], T.hc[:, HA:HA + HL], T.hp[:, HA:HA + HL], True, True))
+    need("s", kw)
+    kwy = s_(S.activation(T.wy[:], T.ps1[:, 0:YV], Act.Copy))
+    need("s", k)
+    k = s_(S.activation(T.vw[:, 1:RW], T.ps0[:, 0:RW - 1], Act.Copy))
+    need("s", k)
+    kvo = s_(S.activation(T.vw[:, 0:3:2], T.ps0[:, HL - 2:HL], Act.Copy))
+
+    cw = T.cw1[:, 15:256:16]
     need("v", kbt, kcw)
     k = v(V.tensor_scalar(T.gr[:], cw, T.bt[:, 0:1], None, Op.add))
     v(V.tensor_scalar(T.z[:], cw, 0.0, T.bt[:, 1:2], Op.is_equal, Op.mult))
@@ -392,41 +440,40 @@ def rank_program(g, core, T, topo):
     k = v(V.tensor_scalar(T.d1[:], T.gr[:], 7, None, Op.bitwise_and))
     need("v", k)
     v(V.tensor_scalar(T.h1[:], T.gi[:], 3, 15, Op.logical_shift_right, Op.bitwise_and))
-    k = v(V.tensor_scalar(T.u[:], T.d1[:], float(RW), 4.0, Op.mult, Op.add))
+    k = v(V.tensor_scalar(T.u[:], T.d1[:], float(RW), 3.0, Op.mult, Op.add))
     need("v", k)
     k = v(V.tensor_tensor(T.u2[:], T.u[:], T.h1[:], Op.add))
+    if r:
+        kn = v(V.tensor_copy(T.nn[:, 0:r], T.ni[:, 0:r]))
     need("v", k)
     k = v(V.tensor_tensor(T.u3[:], T.u2[:], T.z[:], Op.subtract))
+    if r:
+        need("v", kn)
+        kn = v(V.tensor_reduce(T.bt[:, 2:3], T.nn[:, 0:2 * r], AxisListType.X, Op.add))
     need("v", k)
     kpos = v(V.tensor_copy(T.pos[:], T.u3[:]))
     if r:
-        k = v(V.tensor_scalar(T.ni[:, 0:r], T.inf[:, 0:r], 255, None, Op.bitwise_and))
-        v(V.tensor_copy(T.nn[:, r:2 * r], T.sb[:, 0:r]))
-        need("v", k)
-        k = v(V.tensor_copy(T.nn[:, 0:r], T.ni[:, 0:r]))
-        need("v", k)
-        k = v(V.tensor_reduce(T.bt[:, 2:3], T.nn[:, 0:2 * r], AxisListType.X, Op.add))
-        need("v", k)
-        klb = v(V.tensor_scalar(T.lbt[0:1, 256:512], T.cum[0:1, :], T.bt[0:1, 2:3], None, Op.add))
+        need("s", kn)
+        klb = s_(S.activation(T.lbt[0:1, 256:512], T.cum[0:1, :], Act.Identity, bias=T.bt[0:1, 2:3]))
     else:
-        klb = v(V.tensor_copy(T.lbt[0:1, 256:512], T.cum[0:1, :]))
+        klb = s_(S.activation(T.lbt[0:1, 256:512], T.cum[0:1, :], Act.Copy))
     need("y", klb, klb0)
     kslb = inc(Y.dma_start(T.lb[:], T.lbt[0:1, :]), "slb", 16)
 
-    need("t", kvq, khq, ("ar", 4 * len(eng)))
-    kvm = t_(E.matmul_mx(T.ps6[:, 0:NR - RW], T.vc[:], T.vp[:], T.hc[:, HL:HL + NR - RW], T.hp[:, HL:HL + NR - RW], True, True))
+    need("t", kvq, khq, ("ar", 2 * len(eng) + relayed(T, topo, r, 2)))
+    kvm = t_(E.matmul_mx(T.ps6[:, 0:LD + 1], T.vc[:], T.vp[:], T.hc[:, HA + HL:HA + HL + LD + 1], T.hp[:, HA + HL:HA + HL + LD + 1], True, True))
     need("v", kvm)
-    k = v(V.tensor_copy(T.vw[:, RW:NR], T.ps6[:, 0:NR - RW]))
+    k = v(V.tensor_copy(T.vw[:, RW:NR], T.ps6[:, 0:LD]))
     need("s", k, kpos, kvo)
-    kg = s_(S.activation(T.vg[:], T.vw[:].indirect(T.pos[:, 8:16]), Act.Copy))
+    kg = s_(S.activation(T.vg[:], T.vw[:].indirect(T.pos[:, YV // 16:16]), Act.Copy))
     need("v", k, kwy, kpos, kvo)
-    ky0 = v(V.tensor_tensor(T.yt[:, 0:128], T.vw[:].indirect(T.pos[:, 0:8]), T.wy[:], Op.add))
+    ky0 = v(V.tensor_tensor(T.yt[:, 0:YV], T.vw[:].indirect(T.pos[:, 0:YV // 16]), T.wy[:], Op.add))
     need("v", kg)
-    ky1 = v(V.tensor_tensor(T.yt[:, 128:256], T.ps5[:, 128:256], T.vg[:], Op.add))
+    ky1 = v(V.tensor_tensor(T.yt[:, YV:256], T.ps1[:, YV:256], T.vg[:], Op.add))
     need("y", ky0)
-    ks0 = inc(Y.dma_start(T.y[:, 0:128], T.yt[:, 0:128]), "sy0", 16)
+    ks0 = inc(Y.dma_start(T.y[:, 0:YV], T.yt[:, 0:YV]), "sy0", 16)
     need("s", ky1)
-    ks1 = inc(S.dma_start(T.y[:, 128:256], T.yt[:, 128:256]), "sy1", 16)
+    ks1 = inc(S.dma_start(T.y[:, YV:256], T.yt[:, YV:256]), "sy1", 16)
     need("y", kslb, ks0)
     need("s", ks1)
     need("y", k_a, k_w, k_v)

from concourse.bass import DstId, RemoteDMATransfer
from concourse.mybir import dt, AluOpType as Op, AxisListType, ActivationFunctionType as Act

N, TC = 8, 256
EW = 2
W = 17
RW = W + EW
XO = 144
YV = 160
NB, NR = N * W, N * RW
NG = NB // 4
LD = NR - RW
FL, FM = 128, 272
NE = 9
NO = NE + 1
VC, SC = [0, 1, 2, 3], [4, 5, 6, 7, 8]
J0 = 48
BIG = 1e29
RND = 1.5 * 2 ** 23
R12 = RND * 4096
HELP = ((2, 2), (1, 2), (1, 2))
WHOLE = ((0, 0), (1, 0), (1, 1))
NEAR = 3
W1, W2 = RW * (NEAR + 1) + 1, RW * (N - 1 - NEAR) + 2
HA, HL = 512, 256
RELAY = [list(range(1, N)), list(range(1, N - NEAR)), list(range(1, NEAR + 1))]
DIRECT = [[b for b in range(1, N) if b not in bs] for bs in RELAY]

SCRATCH = {}
for _n, _w, _t in (
        ("xs", 1040, "bfloat16"), ("pst", 576, "bfloat16"), ("as_", 2048, "bfloat16"), ("ws", 512, "bfloat16"), ("vsb", 512, "bfloat16"),
        ("tr", 128, "float32"), ("pm", 132, "float32"), ("mk", 64, "float32"), ("nf", 128, "bfloat16"), ("dd", 144, "bfloat16"),
        ("ta", 304, "bfloat16"), ("mh", 128, "bfloat16"), ("bc", 256, "bfloat16"), ("row", 256, "bfloat16"),
        ("df", 256, "bfloat16"), ("sf", 256, "bfloat16"), ("cum", 256, "bfloat16"), ("ones", 256, "bfloat16"),
        ("tp", 4, "float32"), ("msg", 2, "uint16"),
        ("tb", 160, "bfloat16"), ("fi", 160, "bfloat16"), ("th1", NE, "float32"), ("th0", NE, "float32"), ("thr", NE, "float32"), ("te", 1, "float32"),
        ("ss", NE, "float32"), ("sg", 256 * len(SC), "bfloat16"), ("cm", 256 * len(VC), "bfloat16"), ("cs", 256 * len(VC), "bfloat16"),
        ("of", 4 * NO, "uint16"), ("ct", 64 * NE, "bfloat16"), ("q0", NG, "float32"), ("q", NG, "float32"), ("qm", NG, "float32"),
        ("qd", NG, "float32"), ("qe", NG, "float32"), ("b1", NG, "float32"), ("b2", NG, "float32"), ("b3", NG, "float32"), ("b4", NG, "float32"),
        ("b5", NG, "float32"), ("base", NG, "float32"), ("off", NG, "uint16"), ("info", 8, "uint16"), ("inf", 8, "int32"),
        ("la", 8, "int32"), ("fb", 8, "int32"), ("sb", 24, "float32"), ("d0", 24, "float32"), ("so", 24, "float32"),
        ("hs", 4 * NB, "bfloat16"), ("hb", 4 * HL, "bfloat16"),
        ("jm", 256, "bfloat16"), ("mq", 256, "bfloat16"), ("cw1", 256, "bfloat16"),
        ("bt", 4, "float32"), ("gi", 16, "int32"), ("gr", 16, "int32"), ("h1", 16, "int32"), ("d1", 16, "int32"), ("z", 16, "float32"),
        ("u", 16, "float32"), ("u2", 16, "float32"), ("pos", 16, "uint16"), ("u3", 16, "float32"), ("ni", 8, "int32"), ("nn", 16, "float32"),
        ("lbt", 512, "float32"), ("wy", YV, "float32"), ("vw", NR, "float32"), ("vg", 256 - YV, "float32"), ("yt", 256, "float32")):
    SCRATCH[_n] = ("sbuf", [128, _w], _t)
for _n, _m, _w in (("xc", "xp", XO + 256), ("wc", "wp", 128), ("vc", "vp", 128),
                   ("fc", "fp", FM + 128), ("hc", "hp", HA + HL + LD + 2)):
    SCRATCH[_n] = ("sbuf", [128, _w], "float8_e4m3fn_x4")
    SCRATCH[_m] = ("sbuf", [128, _w], "uint8")
for _i in range(8):
    SCRATCH["ps%d" % _i] = ("psum", [128, 512], "float32")
SEMAPHORES = ["v", "s", "t", "gc", "lp", "lxa", "lxb", "la_", "lw", "lv", "inf_", "af", "ar", "loc", "sy0", "sy1", "slb",
              "lc", "in0", "r0", "r1", "r2", "ag", "ae"]


def helpers(core, T, topo):
    near = sorted((c for c in topo.cores_of(core) if c != core), key=lambda c: topo.die(c) != topo.die(core))
    free = [c for c in near if all(topo.may_write(c, d) for d in T.cores if d != core)]
    bound = [c for c in near if c not in free]
    return [[free[what], bound[what]] for what in (0, 1)]


def served(T, topo, r, j, what, i):
    last = helpers(T.cores[r], T, topo)[what][HELP[j][what] - 1]
    return [b for b in RELAY[j] if topo.may_write(last, T.cores[(r + b) % N]) == (i == HELP[j][what] - 1)]


def relayed(T, topo, r, j):
    total = 0
    for b in RELAY[j]:
        s = (r - b) % N
        for what in (0, 1):
            for i in range(HELP[j][what]):
                bs = served(T, topo, s, j, what, i)
                if b in bs:
                    total += shares(topo.engines(T.cores[s], T.cores[r]), len(bs), what)[1][bs.index(b)]
    return total


def steps(T):
    xs, fs, hs = (T.xc, T.xp), (T.fc, T.fp), (T.hc, T.hp)
    return ((xs, lambda b: XO - 1, fs, lambda b: FL + RW * (N - b - 1), RW - W, "ae", "ae"),
            (fs, lambda b: FM + W * (b - 1), fs, lambda b: FL + RW * (N - b) - W, W, "af", "ag"),
            (hs, lambda b: HA + RW * b - 1 + (HL - NR - 1) * (b > NEAR), hs, lambda b: HA + HL + RW * (N - b - 1), RW, "ar", "ar"))


def view(bufs, what, a, w):
    return bufs[1][:, a:a + w] if what else bufs[0][:, a:a + w].bitcast(dt.uint8)


def shares(eng, n, turn):
    size = [1] * n
    while sum(size) + min(size) <= len(eng):
        size[size.index(min(size))] *= 2
    size = size[::-1] if turn else size
    out, at = [], 0
    for k in size:
        out.append(sum(1 << e for e in eng[at:at + k]))
        at += k
    return out, size


def outward(T, topo, core, r, j, what, bs, which):
    src, at, to, land, w = steps(T)[j][:5]
    tr = []
    for b, m in zip(bs, shares(topo.engines(core, T.cores[(r + bs[0]) % N]), len(bs), what)[0]):
        rid, pid = topo.addr(T.cores[(r + b) % N], core)
        tr.append(RemoteDMATransfer(dst_ids=[DstId(rid=rid, pnc=pid)], dma_engine_mask=m, remote_sem=T.sem[steps(T)[j][5 + which]],
                                    srcs=[view(src, what, at(b), w)], dsts=[view(to, what, land(b), w)]))
    return tr


def helper_program(g, core, T, topo, r, what, i):
    out = len(topo.engines(T.cores[r], T.cores[(r + 1) % N]))
    mine = [j for j in range(3) if i < HELP[j][what]]
    for j in mine:
        g.wait_ge(T.sem["r%d" % j], len(topo.engines(T.cores[r], core)) - (0 if WHOLE[j][what] else out))
        g.remote_dma_fused(outward(T, topo, core, r, j, what, served(T, topo, r, j, what, i), 1), local_sem=T.sem.loc)
    g.wait_ge(T.sem.loc, len(mine) * out)


def rank_program(g, core, T, topo):
    r = T.rank_of(core)
    if r is None:
        for i, c in enumerate(T.cores):
            for what, cores in enumerate(helpers(c, T, topo)):
                if core in cores:
                    helper_program(g, core, T, topo, i, what, cores.index(core))
        return
    V, S, E, Y = g.vector, g.scalar, g.tensor, g.sync
    queues = {"v": V, "s": S, "t": E, "y": Y, "g": g}
    cnt, seen = {}, {}

    def inc(ins, sem, n=1):
        ins.then_inc(T.sem[sem], n)
        cnt[sem] = cnt.get(sem, 0) + n
        return (sem, cnt[sem])

    def need(q, *toks):
        best = {}
        for s, n in toks:
            best[s] = max(best.get(s, 0), n)
        for s, n in best.items():
            if seen.get((q, s), 0) < n:
                seen[(q, s)] = n
                queues[q].wait_ge(T.sem[s], n)

    def v(ins): return inc(ins, "v")
    def s_(ins): return inc(ins, "s")
    def t_(ins): return inc(ins, "t")
    def gc(ins): return inc(ins, "gc")

    eng = topo.engines(core, T.cores[(r + 1) % N])
    hlp = helpers(core, T, topo)

    def dst(c):
        rid, pid = topo.addr(c, core)
        return DstId(rid=rid, pnc=pid)

    def inward(j, what):
        src, at, w = steps(T)[j][0], steps(T)[j][1], steps(T)[j][4]
        a, w = at(1), w * (len(RELAY[j]) if j else 1)
        if what and j < 2:
            w = 4 * steps(T)[j][4]
        run = view(src, what, a, w)
        use = [e for e in topo.engines(core, hlp[what][0]) if WHOLE[j][what] or (e in eng) == (j + what == 0)]
        cnt["loc"] = cnt.get("loc", 0) + len(use)
        return [RemoteDMATransfer(dst_ids=[dst(h) for h in hlp[what][:HELP[j][what]]], dma_engine_mask=sum(1 << e for e in use),
                                  remote_sem=T.sem["r%d" % j], srcs=[run], dsts=[run] * HELP[j][what])]

    def direct(j, what):
        cnt["loc"] = cnt.get("loc", 0) + len(eng)
        return outward(T, topo, core, r, j, what, DIRECT[j], 0)

    def send(tok, *calls):
        need("g", tok)
        for tr in calls:
            g.remote_dma_fused(tr, local_sem=T.sem.loc)

    k_p = inc(S.dma_start(T.pst[:, 64:192], T.p[:, 0:128]), "lp", 16)
    k_xa = inc(Y.dma_start(T.xs[:, 0:512], T.x[:, 0:512]), "lxa", 16)
    k_xb = inc(S.dma_start(T.xs[:, 512:1024], T.x[:, 512:1024]), "lxb", 16)

    def iota(out, pattern, base):
        return gc(g.iota(out, pattern, base, 0, allow_small_or_imprecise_dtypes=True))

    for i, (pattern, base) in enumerate((([[0, 2], [1, 16]], 0), ([[0, 2], [1, 4], [0, 4]], 0), ([[0, 8], [1, 4]], 28),
                                         ([[0, 2], [128, 2], [0, 8]], 0), ([[0, 2], [-120, 2], [1, 8]], 241))):
        c_tb = iota(T.tb[:, 32 * i:32 * i + 32], pattern, base)
    c_q0 = iota(T.q0[:], [[4, NG]], 0)
    c_th = iota(T.th0[:], [[16, NE]], -15)
    iota(T.ta[:, 128:144], [[0, 16]], 0)
    c_ta = iota(T.ta[:, 272:304], [[0, 32]], 0)
    Q, Q4, T28, UP, TOP = (T.fi[:, 32 * i:32 * i + 1] for i in range(5))

    kz = v(V.memset(T.pst[:, 0:64], 0.0))
    v(V.memset(T.mk[:], 0.0))
    v(V.memset(T.dd[:], 1.0))
    m1 = v(V.memset(T.mh[:], 0.0))
    v(V.memset(T.pm[:, 0:1], -BIG))
    need("v", m1)
    v(V.memset(T.dd[:, 15:144:32], 18.0))
    v(V.memset(T.mh[:, 0:128:32], -128.0))
    m4 = v(V.memset(T.mk[:, 15:64:16], -BIG))
    v(V.memset(T.df[:, 0:1], 0.0))
    if r:
        v(V.memset(T.sb[:, 2 * r + 2:2 * r + 3], 402653184.0))
        v(V.memset(T.sb[:, 2 * r + 3:2 * r + 4], -402653184.0))
    need("s", k_p)
    cp = [s_(S.activation(T.pst[:, 64 + 128 * k:192 + 128 * k], T.pst[:, 64:192], Act.Copy)) for k in (1,)]
    need("v", c_tb)
    k = v(V.transpose(T.fi[:], T.tb[:]))
    need("s", k, c_q0)
    ks_ = s_(S.activation(T.q[:], T.q0[:], Act.Identity, bias=Q4))
    need("s", ks_)
    s_(S.activation(T.b1[:], T.q[:], Act.Copy, bias=9.0, scale=8.0))
    for out, in_, bias, scale in ((T.qm, T.q, -0.47, 1.0 / W), (T.qd, T.qm, RND, 1.0), (T.qe, T.qd, -RND, 1.0), (T.b2, T.qe, 0.0, 1.0 - 8 * W)):
        need("s", ks_)
        ks_ = s_(S.activation(out[:], in_[:], Act.Copy, bias=bias, scale=scale))
    need("s", c_th)
    k = s_(S.activation(T.th1[:], T.th0[:], Act.Identity, bias=Q))
    need("s", k)
    kthr = s_(S.activation(T.thr[:], T.th1[:], Act.Copy, bias=-0.5))

    need("v", k_p)
    v(V.tensor_copy(T.pst[:, 320:448], T.pst[:, 64:192]))
    k = v(V.tensor_copy(T.pst[:, 448:576], T.pst[:, 64:192]))
    need("v", k, cp[-1], kz)
    v(V.quantize_mx(T.xc[:, 0:XO], T.xp[:, 0:XO], T.pst[:]))
    need("v", k_xa)
    kx0 = v(V.quantize_mx(T.xc[:, XO:XO + 128], T.xp[:, XO:XO + 128], T.xs[:, 0:512]))
    need("v", k_xb)
    kx = v(V.quantize_mx(T.xc[:, XO + 128:], T.xp[:, XO + 128:], T.xs[:, 512:1024]))
    need("t", kx0)
    E.matmul_mx(T.ps0[:, 0:128], T.xc[:, 16:XO], T.xp[:, 16:XO], T.xc[:, XO:XO + 128], T.xp[:, XO:XO + 128], True, False)
    need("t", kx)
    ks = t_(E.matmul_mx(T.ps0[:, 0:128], T.xc[:, 0:128], T.xp[:, 0:128], T.xc[:, XO + 128:], T.xp[:, XO + 128:], False, True))
    need("y", kx0)
    for bufs, a in (((T.fc, T.fp), FL + LD), ((T.hc, T.hp), HA + HL + LD)):
        for what in (0, 1):
            k_c0 = inc(Y.dma_start(view(bufs, what, a, 2), view((T.xc, T.xp), what, XO, 2)), "lc", 16)
    need("y", k_xb)
    k_a = inc(Y.dma_start(T.as_[:], T.a[:]), "la_", 16)
    k_w = inc(Y.dma_start(T.ws[:], T.w[:]), "lw", 16)
    k_v = inc(Y.dma_start(T.vsb[:], T.v[:]), "lv", 16)
    send(kx0, inward(0, 0) + inward(0, 1))
    v(V.memset(T.ones[:], 1.0))

    def halves(after, call):
        done = []
        for h in (0, 1):
            need("v", after[h])
            done.append(v(call(h)))
        return done

    need("v", m4, c_ta)
    k = halves((ks, ks), lambda h: V.transpose(T.tr[:, 64 * h:64 * h + 64], T.ps0[:, 64 * h:64 * h + 64]))
    k = halves(k, lambda h: V.tensor_tensor_scan(T.pm[:, 64 * h + 1:64 * h + 65], T.tr[:, 64 * h:64 * h + 64], T.mk[:], -BIG,
                                                 Op.max, Op.add))
    k = halves(k, lambda h: V.tensor_tensor(T.nf[:, 64 * h:64 * h + 64], T.pm[:, 64 * h:64 * h + 64], T.tr[:, 64 * h:64 * h + 64],
                                            Op.is_ge))
    need("v", ks_)
    kb = v(V.tensor_tensor(T.b3[:], T.b1[:], T.b2[:], Op.add))
    k = halves((k[1], k[1]), lambda h: V.tensor_tensor_scan(T.ta[:, 144 * h:144 * h + 128], T.nf[:], T.dd[:, 16 * h:16 * h + 128], 0.0,
                                                            Op.mult, Op.add))
    k = halves(k, lambda h: V.tensor_tensor_scan(T.bc[:, 128 * h:128 * h + 128], T.mh[:], T.ta[:, 160 * h + 15:160 * h + 143], 0.0,
                                                 Op.add, Op.max))
    k = halves(k, lambda h: V.transpose(T.row[:, 128 * h:128 * h + 128], T.bc[:, 128 * h:128 * h + 128]))
    krow = k[1]
    k = halves(k, lambda h: V.tensor_tensor_scan(T.df[:, 127 * h + 1:128 * h + 128], T.row[:, 127 * h + 1:128 * h + 128],
                                                 T.row[:, 127 * h:128 * h + 127], 0.0, Op.max, Op.subtract))
    k = halves(k, lambda h: V.tensor_scalar(T.sf[:, 128 * h:128 * h + 128], T.df[:, 128 * h:128 * h + 128], 0.0, None, Op.not_equal))
    v(V.tensor_scalar(T.b4[:], T.b3[:], 137.0, None, Op.is_lt))
    need("v", k[1])
    kcum = v(V.tensor_tensor_scan(T.cum[:], T.ones[:], T.sf[:], 0.0, Op.mult, Op.add))
    if r == 1:
        v(V.tensor_scalar(T.tp[:, 2:3], T.row[:, 0:1], 4096.0, R12 - 18.0 * 4096, Op.mult, Op.add))
    elif r:
        v(V.tensor_scalar(T.fb[:, r - 1:r], T.row[:, 0:1], -18.0, None, Op.add))
    need("s", krow)
    first = 256.0 if r else 0.0
    k1 = s_(S.activation(T.tp[:, 0:1], T.row[:, 0:1], Act.Copy, bias=-18.0 * (4096 + first), scale=first))
    need("s", k1)
    ktp = s_(S.activation(T.tp[:, 1:2], T.row[:, 255:256], Act.Identity, bias=T.tp[:, 0:1], scale=4096.0))
    need("v", kcum)
    if r < N - 1:
        need("v", ktp)
        kmsg = v(V.tensor_scalar(T.msg[:, 0:1], T.cum[:, 255:256], T.tp[:, 1:2], None, Op.add))
        need("g", kmsg)
        later = list(range(N - 1, r, -1))
        g.remote_dma_fused([RemoteDMATransfer(dst_ids=[dst(T.cores[d]) for d in later], dma_engine_mask=sum(1 << e for e in eng),
                                              remote_sem=T.sem["inf_" if r else "in0"], srcs=[T.msg[:, 0:1]], dsts=[T.info[:, r:r + 1]] * len(later))],
                           local_sem=T.sem.loc)
        cnt["loc"] += len(eng)
    c_xs = iota(T.xs[:, 1024:1040], [[0, 16]], 0)
    if r:
        iota(T.sb[:, 2 * r:2 * r + 2], [[-14, 2]], 0)
        need("g", iota(T.d0[:], [[0, 24]], 1))
        c_d0 = iota(T.d0[:, 2 * r:2 * r + 1], [[0, 1]], 4)
    c_jm = iota(T.jm[:], [[0, 16], [1, 16]], 0)

    need("s", kcum, kthr)
    for i, c in enumerate(SC):
        kss = s_(S.activation(T.sg[:, 256 * i + J0:256 * i + 256], T.cum[:, J0:256], Act.Sign, bias=T.thr[:, c:c + 1], scale=-1.0,
                              accum_out=T.ss[:, c:c + 1]))
    j0 = [16 * max(c - 1, 0) for c in VC]

    def compare(c, te):
        return v(V.tensor_scalar(T.cm[:, 256 * c + j0[c]:256 * c + 256], T.cum[:, j0[c]:256], te, 2.0, Op.is_lt, Op.mult))

    def count(c):
        return v(V.tensor_tensor_scan(T.cs[:, 256 * c + j0[c]:256 * c + 256], T.ones[:, j0[c]:256], T.cm[:, 256 * c + j0[c]:256 * c + 256],
                                      2.0 * j0[c] - 256 - J0, Op.mult, Op.add))

    need("v", kthr)
    kte = v(V.tensor_scalar(T.te[:], T.cum[:, 255:256], UP, TOP, Op.add, Op.min))
    k1 = compare(1, T.thr[:, 1:2])
    compare(2, T.thr[:, 2:3])
    k3 = compare(3, T.thr[:, 3:4])
    need("v", kte)
    k0 = compare(0, T.te[:])
    need("v", k1)
    count(1)
    need("v", k3)
    count(2)
    count(3)
    need("v", k0)
    k = count(0)
    v(V.tensor_tensor(T.b5[:], T.b3[:], T.b4[:], Op.mult))
    need("v", k)
    kof = []
    for t in range(4):
        for a, b, ss in ((0, len(VC), T.cs[:, 255:256 * len(VC):256]), (len(VC), NE, T.ss[:, len(VC):NE])):
            if a:
                need("v", kss)
            k = v(V.tensor_scalar(T.of[:, NO * t + a:NO * t + b], ss, 2.0, 2.0 * (256 + J0) + t, Op.mult, Op.add))
        kof.append(k)
    need("v", kof[0])
    kbase = v(V.tensor_scalar(T.base[:], T.b5[:], 4.0, T28, Op.mult, Op.add))
    for t in range(4 if r else 2):
        need("s", kof[t], c_xs)
        kcv = kcs = s_(S.activation(T.ct[:, t:64 * NE:4], T.xs[:].indirect(T.of[:, NO * t:NO * t + NE]), Act.Copy))
    for t in range(4 if r else 2, 4):
        need("v", kof[3], c_xs)
        kcv = v(V.tensor_copy(T.ct[:, t:64 * NE:4], T.xs[:].indirect(T.of[:, NO * t:NO * t + NE])))

    if r:
        need("v", c_d0)
        if r == 1:
            need("v", ("in0", len(eng)))
            v(V.tensor_scalar(T.sb[:, 0:1], T.info[:, 0:1], R12, T.tp[:, 2:3], Op.add, Op.not_equal))
            k = v(V.tensor_copy(T.sb[:, 1:2], T.info[:, 0:1]))
        else:
            need("v", ("inf_", (r - 1) * len(eng)))
            k = v(V.tensor_copy(T.inf[:, 1:r], T.info[:, 1:r]))
            need("v", k)
            v(V.tensor_scalar(T.la[:, 1:r], T.inf[:, 1:r], 12, None, Op.logical_shift_right))
            v(V.tensor_scalar(T.fb[:, 0:r - 1], T.inf[:, 1:r], 8, 15, Op.logical_shift_right, Op.bitwise_and))
            need("v", ("in0", len(eng)))
            k = v(V.tensor_scalar(T.la[:, 0:1], T.info[:, 0:1], 1.0 / 4096, None, Op.mult))
            v(V.tensor_copy(T.sb[:, r:2 * r], T.info[:, 0:r]))
            need("v", k)
            k = v(V.tensor_tensor(T.sb[:, 0:r], T.la[:, 0:r], T.fb[:, 0:r], Op.not_equal))
        need("v", k)
        k = v(V.tensor_tensor_scan(T.so[:, 0:2 * r + 4], T.d0[:, 0:2 * r + 4], T.sb[:, 0:2 * r + 4], float(N - r), Op.mult, Op.add))
        need("v", k, kbase)
        koff = v(V.tensor_scalar(T.off[:], T.base[:], T.so[:, 2 * r:2 * r + 1], T.so[:, 2 * r + 3:2 * r + 4], Op.subtract, Op.add))
    else:
        need("v", kbase)
        koff = v(V.tensor_copy(T.off[:], T.base[:]))
    need("s", koff, kcs, kcv)
    kgs = s_(S.activation(T.hs[:, 256:512], T.ct[:].indirect(T.off[:, 16:32]), Act.Copy))
    kgo = s_(S.activation(T.hs[:, 512:4 * NB], T.ct[:].indirect(T.off[:, 32:NG]), Act.Copy))
    need("v", koff, kcs, kcv)
    kgv = v(V.tensor_copy(T.hs[:, 0:256], T.ct[:].indirect(T.off[:, 0:16])))
    need("v", kgs, kgv)
    ksq = v(V.quantize_mx(T.fc[:, FM:FM + 128], T.fp[:, FM:FM + 128], T.hs[:, 0:512]))
    send(ksq, inward(1, 0), inward(1, 1) + direct(1, 0), direct(1, 1))
    kfill = iota(T.hb[:, 4 * W1:4 * (HL - W2)], [[0, 4 * (HL - W1 - W2)]], 0)

    need("v", k_a)
    kaq = v(V.quantize_mx(T.hc[:, 0:HA], T.hp[:, 0:HA], T.as_[:]))
    need("v", kgo)
    kown = v(V.quantize_mx(T.fc[:, 0:FL], T.fp[:, 0:FL], T.hs[:, 4 * (NB - FL):4 * NB]))
    klb0 = s_(S.activation(T.lbt[0:1, 0:256], T.row[0:1, :], Act.Copy, bias=33.0, scale=-1.0))
    need("v", c_jm)
    k = v(V.tensor_scalar(T.mq[:], T.jm[:], Q, 512.0, Op.is_le, Op.mult))
    need("v", k)
    kcw = v(V.tensor_tensor_scan(T.cw1[:], T.mq[:], T.cum[:], 0.0, Op.add, Op.min))

    for wave, (w, at, end, sem) in enumerate(((W1, 0, FL - RW + W1, "af"), (W2, HL - W2, FL + LD + 1, "ag"))):
        need("t", kaq, kown, k_c0, ("ae", relayed(T, topo, r, 0)), (sem, relayed(T, topo, r, 1) if wave else 2 * len(eng)))
        ps = [T["ps%d" % (4 * wave + i)] for i in range(4)]
        km = [t_(E.matmul_mx(ps[i][:, 0:128], T.hc[:, 128 * i:128 * i + 128], T.hp[:, 128 * i:128 * i + 128],
                             T.fc[:, end - 128:end], T.fp[:, end - 128:end], True, True)) for i in range(4)]
        need("v", km[2])
        kh = v(V.tensor_scalar(T.hb[:, 4 * at + 2:4 * (at + w):4], ps[2][:, 128 - w:128], 0.0, 0.05, Op.max, Op.mult))
        for i in (0, 1, 3):
            need("s", km[i])
            khs = s_(S.activation(T.hb[:, 4 * at + i:4 * (at + w):4], ps[i][:, 128 - w:128], Act.Relu, scale=0.05))
        need("v", kh, khs, kfill)
        a = HA + 128 * wave
        khq = v(V.quantize_mx(T.hc[:, a:a + 128], T.hp[:, a:a + 128], T.hb[:, 512 * wave:512 * wave + 512]))
        if wave:
            send(khq, direct(2, 0), direct(2, 1))
        else:
            send(khq, inward(2, 0), inward(2, 1))
    need("v", k_w, k_v)
    kwq = v(V.quantize_mx(T.wc[:], T.wp[:], T.ws[:]))
    kvq = v(V.quantize_mx(T.vc[:], T.vp[:], T.vsb[:]))
    if r:
        k = v(V.tensor_copy(T.inf[:, 0:1], T.info[:, 0:1]))
        v(V.tensor_scalar(T.bt[:, 0:1], T.so[:, 2 * r:2 * r + 1], T.so[:, 2 * r + 3:2 * r + 4], 0.25, Op.subtract, Op.mult))
        kbt = v(V.tensor_scalar(T.bt[:, 1:2], T.sb[:, r - 1:r], -2.0, 3.0, Op.mult, Op.add))
        need("v", k)
        v(V.tensor_scalar(T.ni[:, 0:r], T.inf[:, 0:r], 255, None, Op.bitwise_and))
        v(V.tensor_copy(T.nn[:, r:2 * r], T.sb[:, 0:r]))
    else:
        v(V.memset(T.bt[:, 0:1], 0.0))
        kbt = v(V.memset(T.bt[:, 1:2], 1.0))
    need("t", kwq)
    kw = t_(E.matmul_mx(T.ps1[:, 0:256], T.wc[:], T.wp[:], T.xc[:, XO:], T.xp[:, XO:], True, True))
    need("t", kvq, khq)
    k = t_(E.matmul_mx(T.ps0[:, 0:HL], T.vc[:], T.vp[:], T.hc[:, HA:HA + HL], T.hp[:, HA:HA + HL], True, True))
    need("s", kw)
    kwy = s_(S.activation(T.wy[:], T.ps1[:, 0:YV], Act.Copy))
    need("s", k)
    k = s_(S.activation(T.vw[:, 1:RW], T.ps0[:, 0:RW - 1], Act.Copy))
    need("s", k)
    kvo = s_(S.activation(T.vw[:, 0:3:2], T.ps0[:, HL - 2:HL], Act.Copy))

    cw = T.cw1[:, 15:256:16]
    need("v", kbt, kcw)
    k = v(V.tensor_scalar(T.gr[:], cw, T.bt[:, 0:1], None, Op.add))
    v(V.tensor_scalar(T.z[:], cw, 0.0, T.bt[:, 1:2], Op.is_equal, Op.mult))
    need("v", k)
    v(V.tensor_scalar(T.gi[:], T.gr[:], -1.0, 0.0, Op.add, Op.max))
    k = v(V.tensor_scalar(T.d1[:], T.gr[:], 7, None, Op.bitwise_and))
    need("v", k)
    v(V.tensor_scalar(T.h1[:], T.gi[:], 3, 15, Op.logical_shift_right, Op.bitwise_and))
    k = v(V.tensor_scalar(T.u[:], T.d1[:], float(RW), 3.0, Op.mult, Op.add))
    need("v", k)
    k = v(V.tensor_tensor(T.u2[:], T.u[:], T.h1[:], Op.add))
    if r:
        kn = v(V.tensor_copy(T.nn[:, 0:r], T.ni[:, 0:r]))
    need("v", k)
    k = v(V.tensor_tensor(T.u3[:], T.u2[:], T.z[:], Op.subtract))
    if r:
        need("v", kn)
        kn = v(V.tensor_reduce(T.bt[:, 2:3], T.nn[:, 0:2 * r], AxisListType.X, Op.add))
    need("v", k)
    kpos = v(V.tensor_copy(T.pos[:], T.u3[:]))
    if r:
        need("s", kn)
        klb = s_(S.activation(T.lbt[0:1, 256:512], T.cum[0:1, :], Act.Identity, bias=T.bt[0:1, 2:3]))
    else:
        klb = s_(S.activation(T.lbt[0:1, 256:512], T.cum[0:1, :], Act.Copy))
    need("y", klb, klb0)
    kslb = inc(Y.dma_start(T.lb[:], T.lbt[0:1, :]), "slb", 16)

    need("t", kvq, khq, ("ar", 2 * len(eng) + relayed(T, topo, r, 2)))
    kvm = t_(E.matmul_mx(T.ps6[:, 0:LD + 1], T.vc[:], T.vp[:], T.hc[:, HA + HL:HA + HL + LD + 1], T.hp[:, HA + HL:HA + HL + LD + 1], True, True))
    need("v", kvm)
    k = v(V.tensor_copy(T.vw[:, RW:NR], T.ps6[:, 0:LD]))
    need("s", k, kpos, kvo)
    kg = s_(S.activation(T.vg[:], T.vw[:].indirect(T.pos[:, YV // 16:16]), Act.Copy))
    need("v", k, kwy, kpos, kvo)
    ky0 = v(V.tensor_tensor(T.yt[:, 0:YV], T.vw[:].indirect(T.pos[:, 0:YV // 16]), T.wy[:], Op.add))
    need("v", kg)
    ky1 = v(V.tensor_tensor(T.yt[:, YV:256], T.ps1[:, YV:256], T.vg[:], Op.add))
    need("y", ky0)
    ks0 = inc(Y.dma_start(T.y[:, 0:YV], T.yt[:, 0:YV]), "sy0", 16)
    need("s", ky1)
    ks1 = inc(S.dma_start(T.y[:, YV:256], T.yt[:, YV:256]), "sy1", 16)
    need("y", kslb, ks0)
    need("s", ks1)
    need("y", k_a, k_w, k_v)
    need("g", ("loc", cnt["loc"]))
    for sem in ("gc", "v", "s", "t"):
        need("g", (sem, cnt[sem]))
